import numpy as np
import ml_dtypes


def mxq(x, axis, fmt="e4m3"):
    dtype, down = {"e4m3": (ml_dtypes.float8_e4m3fn, 7), "e5m2": (ml_dtypes.float8_e5m2, 14)}[fmt]
    v = np.moveaxis(np.asarray(x, np.float32).astype(ml_dtypes.bfloat16).astype(np.float64), axis, -1)
    blocks = v.reshape(v.shape[:-1] + (-1, 32))
    amax = np.abs(blocks).max(-1, keepdims=True)
    byte = np.maximum(np.where(amax > 0, np.frexp(amax)[1] - 1 + 127, 0) - down, 1)
    scale = np.exp2(byte - 127.0)
    codes = (blocks / scale).astype(np.float32).astype(dtype).astype(np.float64)
    return np.moveaxis((codes * scale).reshape(v.shape), -1, axis)


WIDE = False


def mx_kscale(k):
    if not WIDE:
        return np.ones(k)
    levels = np.array([10, -10, 5, -5, 0])
    if k % 512:
        return np.exp2(np.random.permutation(np.resize(levels, k // 32))).repeat(32)
    a = np.empty((k // 512, 16))
    for p in range(k // 512):
        a[p, :8] = np.random.permutation(np.resize(levels, 8))
        for g in range(8):
            far = levels[np.abs(levels - a[p, g]) >= 10]
            a[p, g + 8] = far[np.random.randint(len(far))]
    return np.exp2(a.ravel()).repeat(32)


def f64(x):
    return np.asarray(x).astype(np.float64)


def striped(idx):
    return np.tile(idx.reshape(-1, 16).T, (8, 1)).astype(np.uint16)


def unstriped(offs):
    return offs[:16].T.reshape(-1).astype(np.int64)


E2M1 = np.array([0.0, 0.5, 1.0, 1.5, 2.0, 3.0, 4.0, 6.0, -0.0, -0.5, -1.0, -1.5, -2.0, -3.0, -4.0, -6.0])


def pack_fp4(w):
    k, n = w.shape
    w = f64(np.asarray(w, np.float32).astype(ml_dtypes.bfloat16)).reshape(k // 32, 32, n)
    amax = np.abs(w).max(1)
    mant, ex = np.frexp(amax / 6.0)
    byte = np.clip(np.where(amax > 0, np.where(mant > 0.5, ex, ex - 1) + 127, 1), 1, 254)
    scaled = (w * np.exp2(127.0 - byte)[:, None, :]).reshape(k, n).astype(np.float32)
    c = np.ascontiguousarray(scaled.reshape(k // 512, 128, 4, n).transpose(0, 1, 3, 2)).astype(ml_dtypes.float4_e2m1fn).view(np.uint8) & 0xF
    words = (c[..., 0::2] | (c[..., 1::2] << 4)).reshape(k // 512, 128, 2 * n)
    return np.ascontiguousarray(words), np.ascontiguousarray(byte.astype(np.uint8).reshape(k // 512, 16, n))


def unpack_fp4(words, scales):
    g, _, n = scales.shape
    words = np.ascontiguousarray(words).reshape(g, 128, n, 2)
    nib = np.empty((g, 128, n, 4), np.uint8)
    nib[..., 0::2] = words & 0xF
    nib[..., 1::2] = words >> 4
    vals = E2M1[nib] * np.repeat(np.exp2(scales.astype(np.float64) - 127.0), 8, axis=1)[..., None]
    return vals.transpose(0, 1, 3, 2).reshape(g * 512, n)


K, T, S, V, N = 512, 2048, 1024, 512, 128
P = 2 ** 7


def setup_inputs():
    n = np.random.standard_normal
    s = mx_kscale(K)[:, None]
    packed_xT = pack_fp4(n((K, T)) * s)
    return {
        "x_words": packed_xT[0],
        "x_scales": packed_xT[1],
        "w1": (n((K, N)) / np.sqrt(K) / s).astype(np.float32),
        "bound": np.tile(np.random.uniform(0.3, 1.2, V), (P, 1)).astype(np.float32),
        "offs": striped(np.random.permutation(T)[:S]),
        "cen": striped(np.random.permutation(S)[:V]),
        "pos1": striped(np.random.permutation(S)[:V]),
        "pos2": striped(np.random.permutation(S)[:V]),
    }


def reference(x_words, x_scales, w1, bound, offs, cen, pos1, pos2):
    xq = unpack_fp4(x_words, x_scales)[:, unstriped(offs)]
    y = mxq(f64(w1), 0, "e4m3").T @ xq
    yc = y[:, unstriped(cen)]
    low = -1.0 * f64(bound)[:1]
    return yc + (np.maximum(np.minimum(y[:, unstriped(pos1)] - yc, f64(bound)[:1]), low) + np.maximum(np.minimum(y[:, unstriped(pos2)] - yc, f64(bound)[:1]), low)) / 2

@@ -1,0 +1,115 @@
+from contextlib import ExitStack
+
+import concourse.mybir as mybir
+
+K, T, S, V, N = 512, 2048, 1024, 512, 128
+FLOPS = 2 * K * N * S
+
+F32 = mybir.dt.float32
+BF16 = mybir.dt.bfloat16
+I32 = mybir.dt.int32
+U32 = mybir.dt.uint32
+U16 = mybir.dt.uint16
+U8 = mybir.dt.uint8
+FP8X4 = mybir.dt.float8_e4m3fn_x4
+FP4X4 = mybir.dt.float4_e2m1fn_x4
+ALU = mybir.AluOpType
+ACT = mybir.ActivationFunctionType
+
+P = 128
+PIECES = ((0, 256), (256, 256))
+
+
+def tile_picked_huber_none_p_kernel(tc, x_words, x_scales, w1, bound, offs, cen, pos1, pos2, out):
+    nc = tc.nc
+    with ExitStack() as ctx:
+        lists = ctx.enter_context(tc.tile_pool(name="lists", bufs=1))
+        keep = ctx.enter_context(tc.tile_pool(name="keep", bufs=1))
+        psum = ctx.enter_context(tc.psum_pool(name="psum", bufs=1))
+
+        def sb(name, n, dtype=F32):
+            return keep.tile([P, n], dtype, name=name, align_bytes=64)
+
+        offs_t = lists.tile([P, S // 16], U16, name="offs_t")
+        cen_t = lists.tile([P, V // 16], U16, name="cen_t")
+        pos1_t = lists.tile([P, V // 16], U16, name="pos1_t")
+        pos2_t = lists.tile([P, V // 16], U16, name="pos2_t")
+
+        scale_win = sb("scale_win", T, U8)
+        word_win = sb("word_win", T, U16)
+        w_raw = keep.tile([P, 4, N], F32, name="w_raw", align_bytes=64)
+        bound_t = sb("bound_t", V)
+
+        nc.vector.memset(scale_win[:].bitcast(I32), 0)
+        nc.sync.dma_start(word_win[:].bitcast(I32), x_words[0].bitcast(I32))
+        nc.sync.dma_start(offs_t[:], offs)
+        nc.sync.dma_start(w_raw[:], w1.rearrange("(p j) n -> p j n", j=4))
+        nc.sync.dma_start(cen_t[:], cen)
+        nc.sync.dma_start(pos1_t[:], pos1)
+        nc.sync.dma_start(pos2_t[:], pos2)
+        for q in range(4):
+            nc.sync.dma_start(scale_win[32 * q : 32 * q + 4, :].bitcast(I32), x_scales[0, 4 * q : 4 * q + 4, :].bitcast(I32))
+        nc.sync.dma_start(bound_t[:], bound)
+
+        w_bf = keep.tile([P, N, 4], BF16, name="w_bf", align_bytes=64)
+        w_codes = sb("w_codes", N, U32)
+        w_scales = sb("w_scales", N, U8)
+        nc.scalar.activation(w_bf[:], w_raw[:].rearrange("p j n -> p n j"), ACT.Copy)
+
+        words = []
+        for h in range(2):
+            got = sb("words%d" % h, 512, U16)
+            nc.vector.tensor_copy(got[:], word_win[:].indirect(offs_t[:, 32 * h : 32 * h + 32]))
+            words.append(got)
+        nc.vector.quantize_mx(out=w_codes[:].bitcast(FP8X4), scales=w_scales[:], in_=w_bf[:].rearrange("p n j -> p (n j)"))
+
+        y = sb("y", S)
+
+        def product(name, s0, n, scales, c0):
+            acc = psum.tile([P, n], F32, name=name)
+            w0 = s0 % 512
+            nc.tensor.matmul_mx(out=acc[:], lhsT=w_codes[:].bitcast(FP8X4), lhsT_scale=w_scales[:],
+                                rhs=words[s0 // 512][:, w0 : w0 + n].bitcast(FP4X4), rhs_scale=scales[:, c0 : c0 + n], start=True, stop=True)
+            return acc
+
+        for i, (s0, n) in enumerate(((0, 512), (512, 256), (768, 256))):
+            scales = sb("scales%d" % i, n, U8)
+            nc.vector.tensor_copy(scales[:], scale_win[:].indirect(offs_t[:, s0 // 16 : (s0 + n) // 16]))
+            if i < 2:
+                acc = product("acc%d" % i, s0, n, scales, 0)
+                nc.scalar.activation(y[:, s0 : s0 + n], acc[:], ACT.Copy)
+            else:
+                acc = product("acc2", s0, 128, scales, 0)
+                nc.scalar.activation(y[:, s0 : s0 + 128], acc[:], ACT.Copy)
+                acc = product("acc3", s0 + 128, 128, scales, 128)
+                nc.vector.tensor_copy(y[:, s0 + 128 : s0 + 256], acc[:])
+
+        floor = sb("floor", V)
+        nc.scalar.activation(floor[:], bound_t[:], ACT.Copy, scale=-2.0)
+        t = {}
+
+        def step(kind, i):
+            v0, n = PIECES[i]
+            cols = slice(v0, v0 + n)
+            lc = slice(v0 // 16, (v0 + n) // 16)
+            o = sb("%s_%d" % (kind, i), n)
+            t[kind, i] = o
+            if kind == "hi":
+                nc.vector.tensor_tensor(o[:], y[:].indirect(cen_t[:, lc]), bound_t[:, cols], ALU.add)
+            elif kind == "d1":
+                nc.vector.tensor_tensor(o[:], y[:].indirect(pos1_t[:, lc]), t["hi", i][:], ALU.subtract)
+            elif kind == "d2":
+                nc.vector.tensor_tensor(o[:], y[:].indirect(pos2_t[:, lc]), t["hi", i][:], ALU.subtract)
+            elif kind == "m1":
+                nc.vector.scalar_tensor_tensor(o[:], t["d1", i][:], 0.0, floor[:, cols], ALU.min, ALU.max)
+            elif kind == "m2":
+                nc.vector.scalar_tensor_tensor(o[:], t["d2", i][:], 0.0, floor[:, cols], ALU.min, ALU.max)
+            elif kind == "part":
+                nc.vector.scalar_tensor_tensor(o[:], t["m1", i][:], 0.5, t["hi", i][:], ALU.mult, ALU.add)
+            else:
+                nc.vector.scalar_tensor_tensor(o[:], t["m2", i][:], 0.5, t["part", i][:], ALU.mult, ALU.add)
+                nc.sync.dma_start(out[:, cols], o[:])
+
+        for kind, i in (("hi", 0), ("hi", 1), ("d1", 0), ("d2", 0), ("m1", 0), ("m2", 0), ("part", 0), ("d1", 1), ("res", 0),
+                        ("d2", 1), ("m1", 1), ("m2", 1), ("part", 1), ("res", 1)):
+            step(kind, i)

@@ -1,6 +1,7 @@
 from contextlib import ExitStack
 
 import concourse.mybir as mybir
+from concourse.masks import make_identity
 
 K, T, S, V, N = 512, 2048, 1024, 512, 128
 FLOPS = 2 * K * N * S
@@ -17,7 +18,9 @@ ALU = mybir.AluOpType
 ACT = mybir.ActivationFunctionType
 
 P = 128
-PIECES = ((0, 256), (256, 256))
+PACK = 4
+PER_COLUMN = 16
+HALF = S // 2
 
 
 def tile_picked_huber_none_p_kernel(tc, x_words, x_scales, w1, bound, offs, cen, pos1, pos2, out):
@@ -27,89 +30,169 @@ def tile_picked_huber_none_p_kernel(tc, x_words, x_scales, w1, bound, offs, cen,
         keep = ctx.enter_context(tc.tile_pool(name="keep", bufs=1))
         psum = ctx.enter_context(tc.psum_pool(name="psum", bufs=1))
 
-        def sb(name, n, dtype=F32):
-            return keep.tile([P, n], dtype, name=name, align_bytes=64)
+        def sbuf(name, columns, dtype=F32, tag=None):
+            return keep.tile([P, columns], dtype, name=name, tag=tag or name, align_bytes=64)
 
-        offs_t = lists.tile([P, S // 16], U16, name="offs_t")
-        cen_t = lists.tile([P, V // 16], U16, name="cen_t")
-        pos1_t = lists.tile([P, V // 16], U16, name="pos1_t")
-        pos2_t = lists.tile([P, V // 16], U16, name="pos2_t")
+        def entries(list_tile, first, count):
+            return list_tile[:, first // PER_COLUMN : (first + count) // PER_COLUMN]
 
-        scale_win = sb("scale_win", T, U8)
-        word_win = sb("word_win", T, U16)
-        w_raw = keep.tile([P, 4, N], F32, name="w_raw", align_bytes=64)
-        bound_t = sb("bound_t", V)
+        def targets(chunk, chunks=1):
+            return slice(chunk * P, (chunk + chunks) * P)
 
-        nc.vector.memset(scale_win[:].bitcast(I32), 0)
-        nc.sync.dma_start(word_win[:].bitcast(I32), x_words[0].bitcast(I32))
+        offs_t = lists.tile([P, S // PER_COLUMN], U16, name="offs_t")
+        cen_t = lists.tile([P, V // PER_COLUMN], U16, name="cen_t")
+        pos1_t = lists.tile([P, V // PER_COLUMN], U16, name="pos1_t")
+        pos2_t = lists.tile([P, V // PER_COLUMN], U16, name="pos2_t")
+        scale_table = sbuf("scale_table", T, U8)
+        word_table = sbuf("word_table", T, U16)
+        w_raw = keep.tile([P, PACK, N], F32, name="w_raw", align_bytes=64)
+        bound_t = sbuf("bound_t", V)
+        identity = sbuf("identity", P)
+        make_identity(nc, identity[:])
+
+        nc.vector.memset(scale_table[:].bitcast(I32), 0)
+        nc.sync.dma_start(word_table[:].bitcast(I32), x_words[0].bitcast(I32))
         nc.sync.dma_start(offs_t[:], offs)
-        nc.sync.dma_start(w_raw[:], w1.rearrange("(p j) n -> p j n", j=4))
+        nc.sync.dma_start(w_raw[:], w1.rearrange("(p t) n -> p t n", t=PACK))
+        nc.sync.dma_start(bound_t[:], bound)
+        for q in range(4):
+            nc.sync.dma_start(scale_table[32 * q : 32 * q + 4, :].bitcast(I32), x_scales[0, 4 * q : 4 * q + 4, :].bitcast(I32))
         nc.sync.dma_start(cen_t[:], cen)
         nc.sync.dma_start(pos1_t[:], pos1)
         nc.sync.dma_start(pos2_t[:], pos2)
-        for q in range(4):
-            nc.sync.dma_start(scale_win[32 * q : 32 * q + 4, :].bitcast(I32), x_scales[0, 4 * q : 4 * q + 4, :].bitcast(I32))
-        nc.sync.dma_start(bound_t[:], bound)
 
-        w_bf = keep.tile([P, N, 4], BF16, name="w_bf", align_bytes=64)
-        w_codes = sb("w_codes", N, U32)
-        w_scales = sb("w_scales", N, U8)
-        nc.scalar.activation(w_bf[:], w_raw[:].rearrange("p j n -> p n j"), ACT.Copy)
+        w_bf = keep.tile([P, N, PACK], BF16, name="w_bf", align_bytes=64)
+        w_codes = sbuf("w_codes", N, U32)
+        w_scales = sbuf("w_scales", N, U8)
+        nc.scalar.activation(w_bf[:], w_raw[:].rearrange("p t n -> p n t"), ACT.Copy)
+
+        floor = sbuf("floor", V)
+        nc.scalar.activation(floor[:, targets(1, 3)], bound_t[:, targets(1, 3)], ACT.Copy, scale=-2.0)
+        b_col = sbuf("b_col", 2)
+        with nc.allow_non_contiguous_dma(reason="one bound to a partition"):
+            nc.sync.dma_start(b_col[:], bound[0, targets(0, 2)].rearrange("(c p) -> p c", p=P))
+        shift = sbuf("shift", 2)
+        nc.scalar.activation(shift[:, 0:1], b_col[:, 0:1], ACT.Copy, scale=-2.0)
+        nc.scalar.activation(shift[:, 1:2], b_col[:, 1:2], ACT.Copy, scale=-1.0)
 
         words = []
-        for h in range(2):
-            got = sb("words%d" % h, 512, U16)
-            nc.vector.tensor_copy(got[:], word_win[:].indirect(offs_t[:, 32 * h : 32 * h + 32]))
-            words.append(got)
-        nc.vector.quantize_mx(out=w_codes[:].bitcast(FP8X4), scales=w_scales[:], in_=w_bf[:].rearrange("p n j -> p (n j)"))
+        for h in range(S // HALF):
+            picked = sbuf("words%d" % h, HALF, U16)
+            nc.vector.tensor_copy(picked[:], word_table[:].indirect(entries(offs_t, h * HALF, HALF)))
+            words.append(picked)
+        nc.vector.quantize_mx(out=w_codes[:].bitcast(FP8X4), scales=w_scales[:], in_=w_bf[:].rearrange("p n t -> p (n t)"))
 
-        y = sb("y", S)
+        y = sbuf("y", S)
 
-        def product(name, s0, n, scales, c0):
-            acc = psum.tile([P, n], F32, name=name)
-            w0 = s0 % 512
+        def pick_scales(first, count):
+            scales = sbuf("scales%d" % first, count, U8)
+            nc.vector.tensor_copy(scales[:], scale_table[:].indirect(entries(offs_t, first, count)))
+            return scales
+
+        def product(bank, first, count, scales):
+            acc = psum.tile([P, count], F32, name="acc%d" % first, tag=bank)
+            start = first % HALF
             nc.tensor.matmul_mx(out=acc[:], lhsT=w_codes[:].bitcast(FP8X4), lhsT_scale=w_scales[:],
-                                rhs=words[s0 // 512][:, w0 : w0 + n].bitcast(FP4X4), rhs_scale=scales[:, c0 : c0 + n], start=True, stop=True)
+                                rhs=words[first // HALF][:, start : start + count].bitcast(FP4X4), rhs_scale=scales,
+                                start=True, stop=True)
             return acc
 
-        for i, (s0, n) in enumerate(((0, 512), (512, 256), (768, 256))):
-            scales = sb("scales%d" % i, n, U8)
-            nc.vector.tensor_copy(scales[:], scale_win[:].indirect(offs_t[:, s0 // 16 : (s0 + n) // 16]))
-            if i < 2:
-                acc = product("acc%d" % i, s0, n, scales, 0)
-                nc.scalar.activation(y[:, s0 : s0 + n], acc[:], ACT.Copy)
-            else:
-                acc = product("acc2", s0, 128, scales, 0)
-                nc.scalar.activation(y[:, s0 : s0 + 128], acc[:], ACT.Copy)
-                acc = product("acc3", s0 + 128, 128, scales, 128)
-                nc.vector.tensor_copy(y[:, s0 + 128 : s0 + 256], acc[:])
+        for bank, first, count in (("bank0", 0, 512), ("bank1", 512, 256)):
+            acc = product(bank, first, count, pick_scales(first, count)[:])
+            nc.scalar.activation(y[:, first : first + count], acc[:], ACT.Copy)
+        last_scales = pick_scales(768, 256)
+        acc = product("bank2", 768, 128, last_scales[:, 0:128])
+        nc.scalar.activation(y[:, 768:896], acc[:], ACT.Copy)
+        acc = product("bank3", 896, 128, last_scales[:, 128:256])
+        nc.vector.tensor_copy(y[:, 896:1024], acc[:])
 
-        floor = sb("floor", V)
-        nc.scalar.activation(floor[:], bound_t[:], ACT.Copy, scale=-2.0)
-        t = {}
+        neighbours = {1: pos1_t, 2: pos2_t}
+        diff = {d: sbuf("diff%d" % d, V) for d in neighbours}
+        clipped = {d: sbuf("clipped%d" % d, V) for d in neighbours}
+        pull = {d: sbuf("pull%d" % d, 2 * P) for d in neighbours}
+        room = {d: sbuf("room%d" % d, 2 * P) for d in neighbours}
+        base = sbuf("base", 2 * P)
+        partial = sbuf("partial", V)
+        hi, turned, total = {}, {}, {}
 
-        def step(kind, i):
-            v0, n = PIECES[i]
-            cols = slice(v0, v0 + n)
-            lc = slice(v0 // 16, (v0 + n) // 16)
-            o = sb("%s_%d" % (kind, i), n)
-            t[kind, i] = o
-            if kind == "hi":
-                nc.vector.tensor_tensor(o[:], y[:].indirect(cen_t[:, lc]), bound_t[:, cols], ALU.add)
-            elif kind == "d1":
-                nc.vector.tensor_tensor(o[:], y[:].indirect(pos1_t[:, lc]), t["hi", i][:], ALU.subtract)
-            elif kind == "d2":
-                nc.vector.tensor_tensor(o[:], y[:].indirect(pos2_t[:, lc]), t["hi", i][:], ALU.subtract)
-            elif kind == "m1":
-                nc.vector.scalar_tensor_tensor(o[:], t["d1", i][:], 0.0, floor[:, cols], ALU.min, ALU.max)
-            elif kind == "m2":
-                nc.vector.scalar_tensor_tensor(o[:], t["d2", i][:], 0.0, floor[:, cols], ALU.min, ALU.max)
-            elif kind == "part":
-                nc.vector.scalar_tensor_tensor(o[:], t["m1", i][:], 0.5, t["hi", i][:], ALU.mult, ALU.add)
-            else:
-                nc.vector.scalar_tensor_tensor(o[:], t["m2", i][:], 0.5, t["part", i][:], ALU.mult, ALU.add)
-                nc.sync.dma_start(out[:, cols], o[:])
+        def turn(bank, source, start=True, stop=True):
+            nc.tensor.matmul(bank[:], source, identity[:], start=start, stop=stop, is_transpose=True)
 
-        for kind, i in (("hi", 0), ("hi", 1), ("d1", 0), ("d2", 0), ("m1", 0), ("m2", 0), ("part", 0), ("d1", 1), ("res", 0),
-                        ("d2", 1), ("m1", 1), ("m2", 1), ("part", 1), ("res", 1)):
-            step(kind, i)
+        def gather_hi(chunk, chunks, tag):
+            hi[chunk] = sbuf("hi%d" % chunk, chunks * P, tag=tag)
+            nc.vector.tensor_tensor(hi[chunk][:], y[:].indirect(entries(cen_t, chunk * P, chunks * P)),
+                                    bound_t[:, targets(chunk, chunks)], ALU.add)
+
+        def gather_diff(chunk, d, chunks=1):
+            nc.vector.tensor_tensor(diff[d][:, targets(chunk, chunks)],
+                                    y[:].indirect(entries(neighbours[d], chunk * P, chunks * P)), hi[chunk][:], ALU.subtract)
+
+        def make_base(chunk):
+            bank = psum.tile([P, P], F32, name="hi_turned%d" % chunk)
+            turn(bank, hi[chunk][:])
+            nc.scalar.activation(base[:, targets(chunk)], bank[:], ACT.Identity, bias=shift[:, chunk : chunk + 1])
+
+        def turn_diff(chunk, d, bank):
+            turned[chunk, d] = psum.tile([P, P], F32, name="diff_turned%d_%d" % (chunk, d), tag=bank)
+            turn(turned[chunk, d], diff[d][:, targets(chunk)])
+
+        def make_pull(chunk, d):
+            nc.scalar.activation(pull[d][:, targets(chunk)], turned[chunk, d][:], ACT.Relu, scale=-0.5)
+
+        def make_room(chunk, d):
+            nc.scalar.activation(room[d][:, targets(chunk)], pull[d][:, targets(chunk)], ACT.Relu,
+                                 bias=b_col[:, chunk : chunk + 1], scale=-1.0)
+
+        def open_total(chunk):
+            total[chunk] = psum.tile([P, P], F32, name="total%d" % chunk)
+            turn(total[chunk], base[:, targets(chunk)], start=True, stop=False)
+
+        def add_room(chunk, d, last):
+            turn(total[chunk], room[d][:, targets(chunk)], start=False, stop=last)
+
+        def clip(chunk, d, chunks=1):
+            cols = targets(chunk, chunks)
+            nc.vector.scalar_tensor_tensor(clipped[d][:, cols], diff[d][:, cols], 0.0, floor[:, cols], ALU.min, ALU.max)
+
+        def finish(chunk, rest):
+            result = sbuf("result%d" % chunk, P)
+            nc.vector.scalar_tensor_tensor(result[:], clipped[2][:, targets(chunk)], 0.5, rest, ALU.mult, ALU.add)
+            nc.sync.dma_start(out[:, targets(chunk)], result[:])
+
+        gather_hi(0, 1, "hi_outer")
+        gather_hi(1, 1, "hi_inner")
+        make_base(0)
+        gather_diff(0, 1)
+        turn_diff(0, 1, "bank0")
+        make_base(1)
+        make_pull(0, 1)
+        gather_diff(0, 2)
+        turn_diff(0, 2, "bank1")
+        open_total(0)
+        make_pull(0, 2)
+        gather_diff(1, 1)
+        turn_diff(1, 1, "bank3")
+        open_total(1)
+        make_room(0, 1)
+        make_pull(1, 1)
+        make_room(0, 2)
+        add_room(0, 1, last=False)
+        make_room(1, 1)
+        add_room(0, 2, last=True)
+        add_room(1, 1, last=True)
+        result0 = sbuf("result0", P)
+        nc.scalar.activation(result0[:], total[0][:], ACT.Copy)
+        nc.scalar.dma_start(out[:, targets(0)], result0[:])
+
+        gather_diff(1, 2)
+        gather_hi(2, 2, "hi_outer")
+        clip(1, 2)
+        gather_diff(2, 1, chunks=2)
+        gather_diff(2, 2, chunks=2)
+        clip(2, 1, chunks=2)
+        clip(2, 2)
+        nc.vector.scalar_tensor_tensor(partial[:, targets(2, 2)], clipped[1][:, targets(2, 2)], 0.5, hi[2][:], ALU.mult, ALU.add)
+        clip(3, 2)
+        finish(2, partial[:, targets(2)])
+        finish(3, partial[:, targets(3)])
+        finish(1, total[1][:])

@@ -107,34 +107,34 @@ def tile_picked_huber_none_p_kernel(tc, x_words, x_scales, w1, bound, offs, cen,
         nc.vector.tensor_copy(y[:, 896:1024], acc[:])
 
         neighbours = {1: pos1_t, 2: pos2_t}
-        diff = {d: sbuf("diff%d" % d, V) for d in neighbours}
         clipped = {d: sbuf("clipped%d" % d, V) for d in neighbours}
         pull = {d: sbuf("pull%d" % d, 2 * P) for d in neighbours}
         room = {d: sbuf("room%d" % d, 2 * P) for d in neighbours}
         base = sbuf("base", 2 * P)
         partial = sbuf("partial", V)
-        hi, turned, total = {}, {}, {}
+        hi = sbuf("hi", V)
+        diff, turned, total = {}, {}, {}
 
         def turn(bank, source, start=True, stop=True):
             nc.tensor.matmul(bank[:], source, identity[:], start=start, stop=stop, is_transpose=True)
 
-        def gather_hi(chunk, chunks, tag):
-            hi[chunk] = sbuf("hi%d" % chunk, chunks * P, tag=tag)
-            nc.vector.tensor_tensor(hi[chunk][:], y[:].indirect(entries(cen_t, chunk * P, chunks * P)),
-                                    bound_t[:, targets(chunk, chunks)], ALU.add)
+        def gather_hi(chunk, chunks):
+            cols = targets(chunk, chunks)
+            nc.vector.tensor_tensor(hi[:, cols], y[:].indirect(entries(cen_t, chunk * P, chunks * P)), bound_t[:, cols], ALU.add)
 
-        def gather_diff(chunk, d, chunks=1):
-            nc.vector.tensor_tensor(diff[d][:, targets(chunk, chunks)],
-                                    y[:].indirect(entries(neighbours[d], chunk * P, chunks * P)), hi[chunk][:], ALU.subtract)
+        def gather_diff(chunk, d, chunks=1, tag=None):
+            diff[chunk, d] = sbuf("diff%d_%d" % (chunk, d), chunks * P, tag=tag)
+            nc.vector.tensor_tensor(diff[chunk, d][:], y[:].indirect(entries(neighbours[d], chunk * P, chunks * P)),
+                                    hi[:, targets(chunk, chunks)], ALU.subtract)
 
         def make_base(chunk):
             bank = psum.tile([P, P], F32, name="hi_turned%d" % chunk)
-            turn(bank, hi[chunk][:])
+            turn(bank, hi[:, targets(chunk)])
             nc.scalar.activation(base[:, targets(chunk)], bank[:], ACT.Identity, bias=shift[:, chunk : chunk + 1])
 
         def turn_diff(chunk, d, bank):
             turned[chunk, d] = psum.tile([P, P], F32, name="diff_turned%d_%d" % (chunk, d), tag=bank)
-            turn(turned[chunk, d], diff[d][:, targets(chunk)])
+            turn(turned[chunk, d], diff[chunk, d][:])
 
         def make_pull(chunk, d):
             nc.scalar.activation(pull[d][:, targets(chunk)], turned[chunk, d][:], ACT.Relu, scale=-0.5)
@@ -150,49 +150,42 @@ def tile_picked_huber_none_p_kernel(tc, x_words, x_scales, w1, bound, offs, cen,
         def add_room(chunk, d, last):
             turn(total[chunk], room[d][:, targets(chunk)], start=False, stop=last)
 
-        def clip(chunk, d, chunks=1):
+        def clip(chunk, d, chunks):
             cols = targets(chunk, chunks)
-            nc.vector.scalar_tensor_tensor(clipped[d][:, cols], diff[d][:, cols], 0.0, floor[:, cols], ALU.min, ALU.max)
+            nc.vector.scalar_tensor_tensor(clipped[d][:, cols], diff[chunk, d][:], 0.0, floor[:, cols], ALU.min, ALU.max)
 
-        def finish(chunk, rest):
+        def add_half(result, chunk, d, rest):
+            nc.vector.scalar_tensor_tensor(result, clipped[d][:, targets(chunk)], 0.5, rest, ALU.mult, ALU.add)
+
+        def finish(chunk, d, rest):
             result = sbuf("result%d" % chunk, P)
-            nc.vector.scalar_tensor_tensor(result[:], clipped[2][:, targets(chunk)], 0.5, rest, ALU.mult, ALU.add)
+            add_half(result[:], chunk, d, rest)
             nc.sync.dma_start(out[:, targets(chunk)], result[:])
 
-        gather_hi(0, 1, "hi_outer")
-        gather_hi(1, 1, "hi_inner")
+        gather_hi(0, 1)
+        gather_hi(1, 3)
         make_base(0)
-        gather_diff(0, 1)
-        turn_diff(0, 1, "bank0")
         make_base(1)
-        make_pull(0, 1)
-        gather_diff(0, 2)
-        turn_diff(0, 2, "bank1")
+        scalar_pairs = ((0, 1), (0, 2), (1, 1))
+        for (chunk, d), bank in zip(scalar_pairs, ("bank0", "bank1", "bank2")):
+            gather_diff(chunk, d)
+            turn_diff(chunk, d, bank)
+            make_pull(chunk, d)
         open_total(0)
-        make_pull(0, 2)
-        gather_diff(1, 1)
-        turn_diff(1, 1, "bank3")
         open_total(1)
-        make_room(0, 1)
-        make_pull(1, 1)
-        make_room(0, 2)
-        add_room(0, 1, last=False)
-        make_room(1, 1)
-        add_room(0, 2, last=True)
-        add_room(1, 1, last=True)
+        for chunk, d in scalar_pairs:
+            make_room(chunk, d)
+            add_room(chunk, d, last=(chunk, d) != (0, 1))
         result0 = sbuf("result0", P)
         nc.scalar.activation(result0[:], total[0][:], ACT.Copy)
         nc.scalar.dma_start(out[:, targets(0)], result0[:])
 
-        gather_diff(1, 2)
-        gather_hi(2, 2, "hi_outer")
-        clip(1, 2)
-        gather_diff(2, 1, chunks=2)
-        gather_diff(2, 2, chunks=2)
+        gather_diff(1, 2, chunks=3, tag="diff0_1")
+        gather_diff(2, 1, chunks=2, tag="diff0_2")
+        clip(1, 2, chunks=3)
         clip(2, 1, chunks=2)
-        clip(2, 2)
-        nc.vector.scalar_tensor_tensor(partial[:, targets(2, 2)], clipped[1][:, targets(2, 2)], 0.5, hi[2][:], ALU.mult, ALU.add)
-        clip(3, 2)
-        finish(2, partial[:, targets(2)])
-        finish(3, partial[:, targets(3)])
-        finish(1, total[1][:])
+        for chunk in (2, 3):
+            add_half(partial[:, targets(chunk)], chunk, 2, hi[:, targets(chunk)])
+        for chunk in (2, 3):
+            finish(chunk, 1, partial[:, targets(chunk)])
+        finish(1, 2, total[1][:])

@@ -67,13 +67,12 @@ def tile_picked_huber_none_p_kernel(tc, x_words, x_scales, w1, bound, offs, cen,
         nc.scalar.activation(w_bf[:], w_raw[:].rearrange("p t n -> p n t"), ACT.Copy)
 
         floor = sbuf("floor", V)
-        nc.scalar.activation(floor[:, targets(1, 3)], bound_t[:, targets(1, 3)], ACT.Copy, scale=-2.0)
+        nc.scalar.activation(floor[:, targets(2, 2)], bound_t[:, targets(2, 2)], ACT.Copy, scale=-2.0)
         b_col = sbuf("b_col", 2)
         with nc.allow_non_contiguous_dma(reason="one bound to a partition"):
             nc.sync.dma_start(b_col[:], bound[0, targets(0, 2)].rearrange("(c p) -> p c", p=P))
         shift = sbuf("shift", 2)
-        nc.scalar.activation(shift[:, 0:1], b_col[:, 0:1], ACT.Copy, scale=-2.0)
-        nc.scalar.activation(shift[:, 1:2], b_col[:, 1:2], ACT.Copy, scale=-1.0)
+        nc.scalar.activation(shift[:], b_col[:], ACT.Copy, scale=-2.0)
 
         words = []
         for h in range(S // HALF):
@@ -107,85 +106,84 @@ def tile_picked_huber_none_p_kernel(tc, x_words, x_scales, w1, bound, offs, cen,
         nc.vector.tensor_copy(y[:, 896:1024], acc[:])
 
         neighbours = {1: pos1_t, 2: pos2_t}
-        clipped = {d: sbuf("clipped%d" % d, V) for d in neighbours}
-        pull = {d: sbuf("pull%d" % d, 2 * P) for d in neighbours}
-        room = {d: sbuf("room%d" % d, 2 * P) for d in neighbours}
-        base = sbuf("base", 2 * P)
-        partial = sbuf("partial", V)
-        hi = sbuf("hi", V)
-        diff, turned, total = {}, {}, {}
+        hi, diff, clipped, partial, turned, total, pull, room, base = {}, {}, {}, {}, {}, {}, {}, {}, {}
 
         def turn(bank, source, start=True, stop=True):
             nc.tensor.matmul(bank[:], source, identity[:], start=start, stop=stop, is_transpose=True)
 
-        def gather_hi(chunk, chunks):
-            cols = targets(chunk, chunks)
-            nc.vector.tensor_tensor(hi[:, cols], y[:].indirect(entries(cen_t, chunk * P, chunks * P)), bound_t[:, cols], ALU.add)
+        def gather_hi(chunk, tag):
+            hi[chunk] = sbuf("hi%d" % chunk, P, tag=tag)
+            nc.vector.tensor_tensor(hi[chunk][:], y[:].indirect(entries(cen_t, chunk * P, P)), bound_t[:, targets(chunk)], ALU.add)
 
-        def gather_diff(chunk, d, chunks=1, tag=None):
-            diff[chunk, d] = sbuf("diff%d_%d" % (chunk, d), chunks * P, tag=tag)
-            nc.vector.tensor_tensor(diff[chunk, d][:], y[:].indirect(entries(neighbours[d], chunk * P, chunks * P)),
-                                    hi[:, targets(chunk, chunks)], ALU.subtract)
+        def gather_diff(chunk, d):
+            diff[chunk, d] = sbuf("diff%d_%d" % (chunk, d), P)
+            nc.vector.tensor_tensor(diff[chunk, d][:], y[:].indirect(entries(neighbours[d], chunk * P, P)), hi[chunk][:], ALU.subtract)
 
         def make_base(chunk):
             bank = psum.tile([P, P], F32, name="hi_turned%d" % chunk)
-            turn(bank, hi[:, targets(chunk)])
-            nc.scalar.activation(base[:, targets(chunk)], bank[:], ACT.Identity, bias=shift[:, chunk : chunk + 1])
+            turn(bank, hi[chunk][:])
+            base[chunk] = sbuf("base%d" % chunk, P)
+            nc.scalar.activation(base[chunk][:], bank[:], ACT.Identity, bias=shift[:, chunk : chunk + 1])
 
         def turn_diff(chunk, d, bank):
             turned[chunk, d] = psum.tile([P, P], F32, name="diff_turned%d_%d" % (chunk, d), tag=bank)
             turn(turned[chunk, d], diff[chunk, d][:])
 
         def make_pull(chunk, d):
-            nc.scalar.activation(pull[d][:, targets(chunk)], turned[chunk, d][:], ACT.Relu, scale=-0.5)
+            pull[chunk, d] = sbuf("pull%d_%d" % (chunk, d), P)
+            nc.scalar.activation(pull[chunk, d][:], turned[chunk, d][:], ACT.Relu, scale=-0.5)
 
         def make_room(chunk, d):
-            nc.scalar.activation(room[d][:, targets(chunk)], pull[d][:, targets(chunk)], ACT.Relu,
-                                 bias=b_col[:, chunk : chunk + 1], scale=-1.0)
+            room[chunk, d] = sbuf("room%d_%d" % (chunk, d), P)
+            nc.scalar.activation(room[chunk, d][:], pull[chunk, d][:], ACT.Relu, bias=b_col[:, chunk : chunk + 1], scale=-1.0)
 
         def open_total(chunk):
             total[chunk] = psum.tile([P, P], F32, name="total%d" % chunk)
-            turn(total[chunk], base[:, targets(chunk)], start=True, stop=False)
+            turn(total[chunk], base[chunk][:], start=True, stop=False)
 
-        def add_room(chunk, d, last):
-            turn(total[chunk], room[d][:, targets(chunk)], start=False, stop=last)
+        def add_room(chunk, d):
+            turn(total[chunk], room[chunk, d][:], start=False, stop=d == 2)
 
-        def clip(chunk, d, chunks):
-            cols = targets(chunk, chunks)
-            nc.vector.scalar_tensor_tensor(clipped[d][:, cols], diff[chunk, d][:], 0.0, floor[:, cols], ALU.min, ALU.max)
-
-        def add_half(result, chunk, d, rest):
-            nc.vector.scalar_tensor_tensor(result, clipped[d][:, targets(chunk)], 0.5, rest, ALU.mult, ALU.add)
-
-        def finish(chunk, d, rest):
+        def store_total(chunk):
             result = sbuf("result%d" % chunk, P)
-            add_half(result[:], chunk, d, rest)
+            nc.scalar.activation(result[:], total[chunk][:], ACT.Copy)
             nc.sync.dma_start(out[:, targets(chunk)], result[:])
 
-        gather_hi(0, 1)
-        gather_hi(1, 3)
+        gather_hi(0, "hi_even")
+        gather_hi(1, "hi_odd")
         make_base(0)
         make_base(1)
-        scalar_pairs = ((0, 1), (0, 2), (1, 1))
-        for (chunk, d), bank in zip(scalar_pairs, ("bank0", "bank1", "bank2")):
+        pairs = ((0, 1), (0, 2), (1, 1), (1, 2))
+        for (chunk, d), bank in zip(pairs, ("bank0", "bank1", "bank2", "bank3")):
             gather_diff(chunk, d)
             turn_diff(chunk, d, bank)
-            make_pull(chunk, d)
         open_total(0)
         open_total(1)
-        for chunk, d in scalar_pairs:
+        make_pull(*pairs[0])
+        for i, (chunk, d) in enumerate(pairs):
+            if i + 1 < len(pairs):
+                make_pull(*pairs[i + 1])
             make_room(chunk, d)
-            add_room(chunk, d, last=(chunk, d) != (0, 1))
-        result0 = sbuf("result0", P)
-        nc.scalar.activation(result0[:], total[0][:], ACT.Copy)
-        nc.scalar.dma_start(out[:, targets(0)], result0[:])
+            add_room(chunk, d)
+        store_total(0)
+        store_total(1)
 
-        gather_diff(1, 2, chunks=3, tag="diff0_1")
-        gather_diff(2, 1, chunks=2, tag="diff0_2")
-        clip(1, 2, chunks=3)
-        clip(2, 1, chunks=2)
-        for chunk in (2, 3):
-            add_half(partial[:, targets(chunk)], chunk, 2, hi[:, targets(chunk)])
-        for chunk in (2, 3):
-            finish(chunk, 1, partial[:, targets(chunk)])
-        finish(1, 2, total[1][:])
+        late = targets(2, 2)
+        late_hi = sbuf("late_hi", 2 * P, tag="hi_even")
+        late_diff = {d: sbuf("late_diff%d" % d, 2 * P) for d in neighbours}
+        late_clipped = {d: sbuf("late_clipped%d" % d, 2 * P) for d in neighbours}
+        halves = (slice(0, P), slice(P, 2 * P))
+        for chunk, half in zip((2, 3), halves):
+            nc.vector.tensor_tensor(late_hi[:, half], y[:].indirect(entries(cen_t, chunk * P, P)), bound_t[:, targets(chunk)], ALU.add)
+        for chunk, half in zip((2, 3), halves):
+            nc.vector.tensor_tensor(late_diff[1][:, half], y[:].indirect(entries(pos1_t, chunk * P, P)), late_hi[:, half], ALU.subtract)
+        nc.vector.tensor_tensor(late_diff[2][:], y[:].indirect(entries(pos2_t, 2 * P, 2 * P)), late_hi[:], ALU.subtract)
+        for d in neighbours:
+            nc.vector.scalar_tensor_tensor(late_clipped[d][:], late_diff[d][:], 0.0, floor[:, late], ALU.min, ALU.max)
+        late_partial = sbuf("late_partial", 2 * P)
+        for half in halves:
+            nc.vector.scalar_tensor_tensor(late_partial[:, half], late_clipped[1][:, half], 0.5, late_hi[:, half], ALU.mult, ALU.add)
+        for chunk, half in zip((2, 3), halves):
+            result = sbuf("result%d" % chunk, P)
+            nc.vector.scalar_tensor_tensor(result[:], late_clipped[2][:, half], 0.5, late_partial[:, half], ALU.mult, ALU.add)
+            nc.sync.dma_start(out[:, targets(chunk)], result[:])

@@ -44,22 +44,27 @@ def tile_picked_huber_none_p_kernel(tc, x_words, x_scales, w1, bound, offs, cen,
         pos1_t = lists.tile([P, V // PER_COLUMN], U16, name="pos1_t")
         pos2_t = lists.tile([P, V // PER_COLUMN], U16, name="pos2_t")
         scale_table = sbuf("scale_table", T, U8)
+        identity = sbuf("identity", P)
         word_table = sbuf("word_table", T, U16)
+        b_col = sbuf("b_col", 2)
         w_raw = keep.tile([P, PACK, N], F32, name="w_raw", align_bytes=64)
         bound_t = sbuf("bound_t", V)
-        identity = sbuf("identity", P)
-        make_identity(nc, identity[:])
+        plane = sbuf("plane", S, U8)
 
-        nc.vector.memset(scale_table[:].bitcast(I32), 0)
-        nc.sync.dma_start(word_table[:].bitcast(I32), x_words[0].bitcast(I32))
+        nc.vector.memset(scale_table[0:112, :].bitcast(I32), 0)
+        nc.vector.memset(identity[:], 0.0)
+        nc.vector.memset(plane[:].bitcast(I32), 0)
+        make_identity(nc, identity[:], nomemset=True)
+        nc.sync.dma_start(scale_table[112:P, :].bitcast(I32), x_scales[0].bitcast(I32))
         nc.sync.dma_start(offs_t[:], offs)
+        nc.sync.dma_start(word_table[:].bitcast(I32), x_words[0].bitcast(I32))
         nc.sync.dma_start(w_raw[:], w1.rearrange("(p t) n -> p t n", t=PACK))
-        nc.sync.dma_start(bound_t[:], bound)
-        for q in range(4):
-            nc.sync.dma_start(scale_table[32 * q : 32 * q + 4, :].bitcast(I32), x_scales[0, 4 * q : 4 * q + 4, :].bitcast(I32))
         nc.sync.dma_start(cen_t[:], cen)
         nc.sync.dma_start(pos1_t[:], pos1)
         nc.sync.dma_start(pos2_t[:], pos2)
+        nc.sync.dma_start(bound_t[:], bound)
+        with nc.allow_non_contiguous_dma(reason="one bound to a partition"):
+            nc.sync.dma_start(b_col[:], bound[0, targets(0, 2)].rearrange("(c p) -> p c", p=P))
 
         w_bf = keep.tile([P, N, PACK], BF16, name="w_bf", align_bytes=64)
         w_codes = sbuf("w_codes", N, U32)
@@ -68,42 +73,34 @@ def tile_picked_huber_none_p_kernel(tc, x_words, x_scales, w1, bound, offs, cen,
 
         floor = sbuf("floor", V)
         nc.scalar.activation(floor[:, targets(2, 2)], bound_t[:, targets(2, 2)], ACT.Copy, scale=-2.0)
-        b_col = sbuf("b_col", 2)
-        with nc.allow_non_contiguous_dma(reason="one bound to a partition"):
-            nc.sync.dma_start(b_col[:], bound[0, targets(0, 2)].rearrange("(c p) -> p c", p=P))
         shift = sbuf("shift", 2)
         nc.scalar.activation(shift[:], b_col[:], ACT.Copy, scale=-2.0)
 
-        words = []
         for h in range(S // HALF):
-            picked = sbuf("words%d" % h, HALF, U16)
-            nc.vector.tensor_copy(picked[:], word_table[:].indirect(entries(offs_t, h * HALF, HALF)))
-            words.append(picked)
-        nc.vector.quantize_mx(out=w_codes[:].bitcast(FP8X4), scales=w_scales[:], in_=w_bf[:].rearrange("p n t -> p (n t)"))
+            picked = sbuf("scales%d" % h, HALF, U8)
+            nc.vector.tensor_copy(picked[:], scale_table[:].indirect(entries(offs_t, h * HALF, HALF)))
+            for r in range(4):
+                nc.sync.dma_start(plane[r:P:32, h * HALF : (h + 1) * HALF].bitcast(I32), picked[112 + r : P : 4, :].bitcast(I32))
 
         y = sbuf("y", S)
+        words = [sbuf("words0", HALF, U16)]
+        nc.vector.tensor_copy(words[0][:], word_table[:].indirect(entries(offs_t, 0, HALF)))
+        nc.vector.quantize_mx(out=w_codes[:].bitcast(FP8X4), scales=w_scales[:], in_=w_bf[:].rearrange("p n t -> p (n t)"))
+        words.append(sbuf("words1", HALF, U16, tag="w_bf"))
 
-        def pick_scales(first, count):
-            scales = sbuf("scales%d" % first, count, U8)
-            nc.vector.tensor_copy(scales[:], scale_table[:].indirect(entries(offs_t, first, count)))
-            return scales
-
-        def product(bank, first, count, scales):
+        def product(bank, first, count):
             acc = psum.tile([P, count], F32, name="acc%d" % first, tag=bank)
-            start = first % HALF
+            cols = slice(first % HALF, first % HALF + count)
             nc.tensor.matmul_mx(out=acc[:], lhsT=w_codes[:].bitcast(FP8X4), lhsT_scale=w_scales[:],
-                                rhs=words[first // HALF][:, start : start + count].bitcast(FP4X4), rhs_scale=scales,
+                                rhs=words[first // HALF][:, cols].bitcast(FP4X4), rhs_scale=plane[:, first : first + count],
                                 start=True, stop=True)
             return acc
 
-        for bank, first, count in (("bank0", 0, 512), ("bank1", 512, 256)):
-            acc = product(bank, first, count, pick_scales(first, count)[:])
-            nc.scalar.activation(y[:, first : first + count], acc[:], ACT.Copy)
-        last_scales = pick_scales(768, 256)
-        acc = product("bank2", 768, 128, last_scales[:, 0:128])
-        nc.scalar.activation(y[:, 768:896], acc[:], ACT.Copy)
-        acc = product("bank3", 896, 128, last_scales[:, 128:256])
-        nc.vector.tensor_copy(y[:, 896:1024], acc[:])
+        for first in (512, 768):
+            nc.vector.tensor_copy(words[1][:, first - HALF : first - HALF + 256], word_table[:].indirect(entries(offs_t, first, 256)))
+        for bank, first, count in (("bank0", 0, 256), ("bank1", 256, 256), ("bank4", 512, 256), ("bank2", 768, 128)):
+            nc.scalar.activation(y[:, first : first + count], product(bank, first, count)[:], ACT.Copy)
+        nc.vector.tensor_copy(y[:, 896:1024], product("bank3", 896, 128)[:])
 
         neighbours = {1: pos1_t, 2: pos2_t}
         hi, diff, clipped, partial, turned, total, pull, room, base = {}, {}, {}, {}, {}, {}, {}, {}, {}
@@ -120,7 +117,7 @@ def tile_picked_huber_none_p_kernel(tc, x_words, x_scales, w1, bound, offs, cen,
             nc.vector.tensor_tensor(diff[chunk, d][:], y[:].indirect(entries(neighbours[d], chunk * P, P)), hi[chunk][:], ALU.subtract)
 
         def make_base(chunk):
-            bank = psum.tile([P, P], F32, name="hi_turned%d" % chunk)
+            bank = psum.tile([P, P], F32, name="hi_turned%d" % chunk, tag="bank%d" % chunk)
             turn(bank, hi[chunk][:])
             base[chunk] = sbuf("base%d" % chunk, P)
             nc.scalar.activation(base[chunk][:], bank[:], ACT.Identity, bias=shift[:, chunk : chunk + 1])
@@ -154,7 +151,7 @@ def tile_picked_huber_none_p_kernel(tc, x_words, x_scales, w1, bound, offs, cen,
         make_base(0)
         make_base(1)
         pairs = ((0, 1), (0, 2), (1, 1), (1, 2))
-        for (chunk, d), bank in zip(pairs, ("bank0", "bank1", "bank2", "bank3")):
+        for (chunk, d), bank in zip(pairs, ("bank4", "bank2", "bank3", "bank5")):
             gather_diff(chunk, d)
             turn_diff(chunk, d, bank)
         open_total(0)

@@ -52,16 +52,15 @@ def tile_picked_huber_none_p_kernel(tc, x_words, x_scales, w1, bound, offs, cen,
         plane = sbuf("plane", S, U8)
 
         nc.vector.memset(scale_table[0:112, :].bitcast(I32), 0)
-        nc.vector.memset(identity[:], 0.0)
         nc.vector.memset(plane[:].bitcast(I32), 0)
-        make_identity(nc, identity[:], nomemset=True)
+        make_identity(nc, identity[:])
         nc.sync.dma_start(scale_table[112:P, :].bitcast(I32), x_scales[0].bitcast(I32))
         nc.sync.dma_start(offs_t[:], offs)
-        nc.sync.dma_start(word_table[:].bitcast(I32), x_words[0].bitcast(I32))
-        nc.sync.dma_start(w_raw[:], w1.rearrange("(p t) n -> p t n", t=PACK))
         nc.sync.dma_start(cen_t[:], cen)
         nc.sync.dma_start(pos1_t[:], pos1)
         nc.sync.dma_start(pos2_t[:], pos2)
+        nc.sync.dma_start(word_table[:].bitcast(I32), x_words[0].bitcast(I32))
+        nc.sync.dma_start(w_raw[:], w1.rearrange("(p t) n -> p t n", t=PACK))
         nc.sync.dma_start(bound_t[:], bound)
         with nc.allow_non_contiguous_dma(reason="one bound to a partition"):
             nc.sync.dma_start(b_col[:], bound[0, targets(0, 2)].rearrange("(c p) -> p c", p=P))
@@ -76,11 +75,11 @@ def tile_picked_huber_none_p_kernel(tc, x_words, x_scales, w1, bound, offs, cen,
         shift = sbuf("shift", 2)
         nc.scalar.activation(shift[:], b_col[:], ACT.Copy, scale=-2.0)
 
-        for h in range(S // HALF):
-            picked = sbuf("scales%d" % h, HALF, U8)
-            nc.vector.tensor_copy(picked[:], scale_table[:].indirect(entries(offs_t, h * HALF, HALF)))
+        for first, count in ((0, 640), (640, 384)):
+            picked = sbuf("scales%d" % first, count, U8)
+            nc.vector.tensor_copy(picked[:], scale_table[:].indirect(entries(offs_t, first, count)))
             for r in range(4):
-                nc.sync.dma_start(plane[r:P:32, h * HALF : (h + 1) * HALF].bitcast(I32), picked[112 + r : P : 4, :].bitcast(I32))
+                nc.sync.dma_start(plane[r:P:32, first : first + count].bitcast(I32), picked[112 + r : P : 4, :].bitcast(I32))
 
         y = sbuf("y", S)
         words = [sbuf("words0", HALF, U16)]
@@ -98,9 +97,10 @@ def tile_picked_huber_none_p_kernel(tc, x_words, x_scales, w1, bound, offs, cen,
 
         for first in (512, 768):
             nc.vector.tensor_copy(words[1][:, first - HALF : first - HALF + 256], word_table[:].indirect(entries(offs_t, first, 256)))
-        for bank, first, count in (("bank0", 0, 256), ("bank1", 256, 256), ("bank4", 512, 256), ("bank2", 768, 128)):
+        for bank, first, count in (("bank0", 0, 256), ("bank1", 256, 256), ("bank4", 512, 128), ("bank5", 640, 128), ):
             nc.scalar.activation(y[:, first : first + count], product(bank, first, count)[:], ACT.Copy)
-        nc.vector.tensor_copy(y[:, 896:1024], product("bank3", 896, 128)[:])
+        nc.vector.tensor_copy(y[:, 768:896], product("bank2", 768, 128)[:])
+        nc.scalar.activation(y[:, 896:1024], product("bank3", 896, 128)[:], ACT.Copy)
 
         neighbours = {1: pos1_t, 2: pos2_t}
         hi, diff, clipped, partial, turned, total, pull, room, base = {}, {}, {}, {}, {}, {}, {}, {}, {}

@@ -54,7 +54,7 @@ def tile_picked_huber_none_p_kernel(tc, x_words, x_scales, w1, bound, offs, cen,
         nc.vector.memset(scale_table[0:112, :].bitcast(I32), 0)
         nc.vector.memset(plane[:].bitcast(I32), 0)
         make_identity(nc, identity[:])
-        nc.sync.dma_start(scale_table[112:P, :].bitcast(I32), x_scales[0].bitcast(I32))
+        nc.scalar.dma_start(scale_table[112:P, :].bitcast(I32), x_scales[0].bitcast(I32))
         nc.sync.dma_start(offs_t[:], offs)
         nc.sync.dma_start(cen_t[:], cen)
         nc.sync.dma_start(pos1_t[:], pos1)
@@ -109,7 +109,7 @@ def tile_picked_huber_none_p_kernel(tc, x_words, x_scales, w1, bound, offs, cen,
             nc.tensor.matmul(bank[:], source, identity[:], start=start, stop=stop, is_transpose=True)
 
         def gather_hi(chunk, tag):
-            hi[chunk] = sbuf("hi%d" % chunk, P, tag=tag)
+            hi[chunk] = early_hi[:, targets(chunk)]
             nc.vector.tensor_tensor(hi[chunk][:], y[:].indirect(entries(cen_t, chunk * P, P)), bound_t[:, targets(chunk)], ALU.add)
 
         def gather_diff(chunk, d):
@@ -146,14 +146,20 @@ def tile_picked_huber_none_p_kernel(tc, x_words, x_scales, w1, bound, offs, cen,
             nc.scalar.activation(result[:], total[chunk][:], ACT.Copy)
             nc.sync.dma_start(out[:, targets(chunk)], result[:])
 
+        early_hi = sbuf("early_hi", 2 * P)
         gather_hi(0, "hi_even")
         gather_hi(1, "hi_odd")
         make_base(0)
         make_base(1)
-        pairs = ((0, 1), (0, 2), (1, 1), (1, 2))
-        for (chunk, d), bank in zip(pairs, ("bank4", "bank2", "bank3", "bank5")):
-            gather_diff(chunk, d)
-            turn_diff(chunk, d, bank)
+        pairs = ((0, 1), (1, 1), (0, 2), (1, 2))
+        for chunk, bank in ((0, "bank4"), (1, "bank2")):
+            gather_diff(chunk, 1)
+            turn_diff(chunk, 1, bank)
+        both = sbuf("diff_second", 2 * P)
+        nc.vector.tensor_tensor(both[:], y[:].indirect(entries(pos2_t, 0, 2 * P)), early_hi[:], ALU.subtract)
+        for chunk, bank in ((0, "bank3"), (1, "bank5")):
+            diff[chunk, 2] = both[:, targets(chunk)]
+            turn_diff(chunk, 2, bank)
         open_total(0)
         open_total(1)
         make_pull(*pairs[0])
@@ -166,7 +172,7 @@ def tile_picked_huber_none_p_kernel(tc, x_words, x_scales, w1, bound, offs, cen,
         store_total(1)
 
         late = targets(2, 2)
-        late_hi = sbuf("late_hi", 2 * P, tag="hi_even")
+        late_hi = sbuf("late_hi", 2 * P, tag="diff0_1")
         late_diff = {d: sbuf("late_diff%d" % d, 2 * P) for d in neighbours}
         late_clipped = {d: sbuf("late_clipped%d" % d, 2 * P) for d in neighbours}
         halves = (slice(0, P), slice(P, 2 * P))

@@ -54,7 +54,7 @@ def tile_picked_huber_none_p_kernel(tc, x_words, x_scales, w1, bound, offs, cen,
         nc.vector.memset(scale_table[0:112, :].bitcast(I32), 0)
         nc.vector.memset(plane[:].bitcast(I32), 0)
         make_identity(nc, identity[:])
-        nc.scalar.dma_start(scale_table[112:P, :].bitcast(I32), x_scales[0].bitcast(I32))
+        nc.sync.dma_start(scale_table[112:P, :].bitcast(I32), x_scales[0].bitcast(I32))
         nc.sync.dma_start(offs_t[:], offs)
         nc.sync.dma_start(cen_t[:], cen)
         nc.sync.dma_start(pos1_t[:], pos1)

@@ -47,7 +47,7 @@ def tile_picked_huber_none_p_kernel(tc, x_words, x_scales, w1, bound, offs, cen,
         identity = sbuf("identity", P)
         word_table = sbuf("word_table", T, U16)
         b_col = sbuf("b_col", 2)
-        w_raw = keep.tile([P, PACK, N], F32, name="w_raw", align_bytes=64)
+        w_raw = keep.tile([P, PACK, N], F32, name="w_raw", tag="w_raw", align_bytes=64)
         bound_t = sbuf("bound_t", V)
         plane = sbuf("plane", S, U8)
 
@@ -85,7 +85,7 @@ def tile_picked_huber_none_p_kernel(tc, x_words, x_scales, w1, bound, offs, cen,
         words = [sbuf("words0", HALF, U16)]
         nc.vector.tensor_copy(words[0][:], word_table[:].indirect(entries(offs_t, 0, HALF)))
         nc.vector.quantize_mx(out=w_codes[:].bitcast(FP8X4), scales=w_scales[:], in_=w_bf[:].rearrange("p n t -> p (n t)"))
-        words.append(sbuf("words1", HALF, U16, tag="w_bf"))
+        words.append(sbuf("words1", HALF, U16, tag="w_raw"))
 
         def product(bank, first, count):
             acc = psum.tile([P, count], F32, name="acc%d" % first, tag=bank)

@@ -46,7 +46,7 @@ def tile_picked_huber_none_p_kernel(tc, x_words, x_scales, w1, bound, offs, cen,
         scale_table = sbuf("scale_table", T, U8)
         identity = sbuf("identity", P)
         word_table = sbuf("word_table", T, U16)
-        b_col = sbuf("b_col", 2)
+        b_col = sbuf("b_col", 3)
         w_raw = keep.tile([P, PACK, N], F32, name="w_raw", tag="w_raw", align_bytes=64)
         bound_t = sbuf("bound_t", V)
         plane = sbuf("plane", S, U8)
@@ -56,14 +56,14 @@ def tile_picked_huber_none_p_kernel(tc, x_words, x_scales, w1, bound, offs, cen,
         make_identity(nc, identity[:])
         nc.sync.dma_start(scale_table[112:P, :].bitcast(I32), x_scales[0].bitcast(I32))
         nc.sync.dma_start(offs_t[:], offs)
-        nc.sync.dma_start(cen_t[:], cen)
-        nc.sync.dma_start(pos1_t[:], pos1)
-        nc.sync.dma_start(pos2_t[:], pos2)
         nc.sync.dma_start(word_table[:].bitcast(I32), x_words[0].bitcast(I32))
         nc.sync.dma_start(w_raw[:], w1.rearrange("(p t) n -> p t n", t=PACK))
         nc.sync.dma_start(bound_t[:], bound)
+        nc.sync.dma_start(cen_t[:], cen)
+        nc.sync.dma_start(pos1_t[:], pos1)
+        nc.sync.dma_start(pos2_t[:], pos2)
         with nc.allow_non_contiguous_dma(reason="one bound to a partition"):
-            nc.sync.dma_start(b_col[:], bound[0, targets(0, 2)].rearrange("(c p) -> p c", p=P))
+            nc.sync.dma_start(b_col[:], bound[0, targets(0, 3)].rearrange("(c p) -> p c", p=P))
 
         w_bf = keep.tile([P, N, PACK], BF16, name="w_bf", align_bytes=64)
         w_codes = sbuf("w_codes", N, U32)
@@ -71,9 +71,13 @@ def tile_picked_huber_none_p_kernel(tc, x_words, x_scales, w1, bound, offs, cen,
         nc.scalar.activation(w_bf[:], w_raw[:].rearrange("p t n -> p n t"), ACT.Copy)
 
         floor = sbuf("floor", V)
-        nc.scalar.activation(floor[:, targets(2, 2)], bound_t[:, targets(2, 2)], ACT.Copy, scale=-2.0)
-        shift = sbuf("shift", 2)
-        nc.scalar.activation(shift[:], b_col[:], ACT.Copy, scale=-2.0)
+        nc.scalar.activation(floor[:, targets(1, 3)], bound_t[:, targets(1, 3)], ACT.Copy, scale=-2.0)
+        hi = sbuf("hi", V)
+        mixed = sbuf("mixed", 2 * P)
+        shift2 = sbuf("shift2", 1)
+        shift = [hi[:, 3 * P : 3 * P + 1], mixed[:, 0:1], shift2[:]]
+        for chunk, rooms in enumerate((2, 1, 1)):
+            nc.scalar.activation(shift[chunk], b_col[:, chunk : chunk + 1], ACT.Copy, scale=-1.0 * rooms)
 
         for first, count in ((0, 640), (640, 384)):
             picked = sbuf("scales%d" % first, count, U8)
@@ -102,91 +106,75 @@ def tile_picked_huber_none_p_kernel(tc, x_words, x_scales, w1, bound, offs, cen,
         nc.vector.tensor_copy(y[:, 768:896], product("bank2", 768, 128)[:])
         nc.scalar.activation(y[:, 896:1024], product("bank3", 896, 128)[:], ACT.Copy)
 
-        neighbours = {1: pos1_t, 2: pos2_t}
-        hi, diff, clipped, partial, turned, total, pull, room, base = {}, {}, {}, {}, {}, {}, {}, {}, {}
-
         def turn(bank, source, start=True, stop=True):
-            nc.tensor.matmul(bank[:], source, identity[:], start=start, stop=stop, is_transpose=True)
+            nc.tensor.matmul(bank, source, identity[:], start=start, stop=stop, is_transpose=True)
 
-        def gather_hi(chunk, tag):
-            hi[chunk] = early_hi[:, targets(chunk)]
-            nc.vector.tensor_tensor(hi[chunk][:], y[:].indirect(entries(cen_t, chunk * P, P)), bound_t[:, targets(chunk)], ALU.add)
+        def gather(into, list_tile, chunk, chunks, other, op):
+            nc.vector.tensor_tensor(into, y[:].indirect(entries(list_tile, chunk * P, chunks * P)), other, op)
 
-        def gather_diff(chunk, d):
-            diff[chunk, d] = sbuf("diff%d_%d" % (chunk, d), P)
-            nc.vector.tensor_tensor(diff[chunk, d][:], y[:].indirect(entries(neighbours[d], chunk * P, P)), hi[chunk][:], ALU.subtract)
+        def relu(name, source, columns, **affine):
+            made = sbuf(name, columns)
+            nc.scalar.activation(made[:], source, ACT.Relu, **affine)
+            return made
 
-        def make_base(chunk):
-            bank = psum.tile([P, P], F32, name="hi_turned%d" % chunk, tag="bank%d" % chunk)
-            turn(bank, hi[chunk][:])
-            base[chunk] = sbuf("base%d" % chunk, P)
-            nc.scalar.activation(base[chunk][:], bank[:], ACT.Identity, bias=shift[:, chunk : chunk + 1])
+        def turned(name, bank, source, chunks):
+            held = psum.tile([P, chunks * P], F32, name=name, tag=bank)
+            for i in range(chunks):
+                turn(held[:, targets(i)], source[:, targets(i)])
+            return held
 
-        def turn_diff(chunk, d, bank):
-            turned[chunk, d] = psum.tile([P, P], F32, name="diff_turned%d_%d" % (chunk, d), tag=bank)
-            turn(turned[chunk, d], diff[chunk, d][:])
+        def open_total(chunk, centres, bank, total_bank):
+            base = sbuf("base%d" % chunk, P)
+            nc.scalar.activation(base[:], turned("hi_turned%d" % chunk, bank, centres, 1)[:], ACT.Identity, bias=shift[chunk])
+            total = psum.tile([P, P], F32, name="total%d" % chunk, tag=total_bank)
+            turn(total[:], base[:], start=True, stop=False)
+            return total
 
-        def make_pull(chunk, d):
-            pull[chunk, d] = sbuf("pull%d_%d" % (chunk, d), P)
-            nc.scalar.activation(pull[chunk, d][:], turned[chunk, d][:], ACT.Relu, scale=-0.5)
+        def add_room(name, chunk, pull, total, last):
+            room = relu(name, pull, P, bias=b_col[:, chunk : chunk + 1], scale=-1.0)
+            turn(total[:], room[:], start=False, stop=last)
 
-        def make_room(chunk, d):
-            room[chunk, d] = sbuf("room%d_%d" % (chunk, d), P)
-            nc.scalar.activation(room[chunk, d][:], pull[chunk, d][:], ACT.Relu, bias=b_col[:, chunk : chunk + 1], scale=-1.0)
-
-        def open_total(chunk):
-            total[chunk] = psum.tile([P, P], F32, name="total%d" % chunk)
-            turn(total[chunk], base[chunk][:], start=True, stop=False)
-
-        def add_room(chunk, d):
-            turn(total[chunk], room[chunk, d][:], start=False, stop=d == 2)
-
-        def store_total(chunk):
+        def store_total(chunk, total):
             result = sbuf("result%d" % chunk, P)
-            nc.scalar.activation(result[:], total[chunk][:], ACT.Copy)
+            nc.scalar.activation(result[:], total[:], ACT.Copy)
             nc.sync.dma_start(out[:, targets(chunk)], result[:])
 
-        early_hi = sbuf("early_hi", 2 * P)
-        gather_hi(0, "hi_even")
-        gather_hi(1, "hi_odd")
-        make_base(0)
-        make_base(1)
-        pairs = ((0, 1), (1, 1), (0, 2), (1, 2))
-        for chunk, bank in ((0, "bank4"), (1, "bank2")):
-            gather_diff(chunk, 1)
-            turn_diff(chunk, 1, bank)
-        both = sbuf("diff_second", 2 * P)
-        nc.vector.tensor_tensor(both[:], y[:].indirect(entries(pos2_t, 0, 2 * P)), early_hi[:], ALU.subtract)
-        for chunk, bank in ((0, "bank3"), (1, "bank5")):
-            diff[chunk, 2] = both[:, targets(chunk)]
-            turn_diff(chunk, 2, bank)
-        open_total(0)
-        open_total(1)
-        make_pull(*pairs[0])
-        for i, (chunk, d) in enumerate(pairs):
-            if i + 1 < len(pairs):
-                make_pull(*pairs[i + 1])
-            make_room(chunk, d)
-            add_room(chunk, d)
-        store_total(0)
-        store_total(1)
+        def fused(into, first, scalar, second, op0, op1):
+            nc.vector.scalar_tensor_tensor(into, first, scalar, second, op0, op1)
 
-        late = targets(2, 2)
-        late_hi = sbuf("late_hi", 2 * P, tag="diff0_1")
-        late_diff = {d: sbuf("late_diff%d" % d, 2 * P) for d in neighbours}
-        late_clipped = {d: sbuf("late_clipped%d" % d, 2 * P) for d in neighbours}
-        halves = (slice(0, P), slice(P, 2 * P))
-        for chunk, half in zip((2, 3), halves):
-            nc.vector.tensor_tensor(late_hi[:, half], y[:].indirect(entries(cen_t, chunk * P, P)), bound_t[:, targets(chunk)], ALU.add)
-        for chunk, half in zip((2, 3), halves):
-            nc.vector.tensor_tensor(late_diff[1][:, half], y[:].indirect(entries(pos1_t, chunk * P, P)), late_hi[:, half], ALU.subtract)
-        nc.vector.tensor_tensor(late_diff[2][:], y[:].indirect(entries(pos2_t, 2 * P, 2 * P)), late_hi[:], ALU.subtract)
-        for d in neighbours:
-            nc.vector.scalar_tensor_tensor(late_clipped[d][:], late_diff[d][:], 0.0, floor[:, late], ALU.min, ALU.max)
-        late_partial = sbuf("late_partial", 2 * P)
-        for half in halves:
-            nc.vector.scalar_tensor_tensor(late_partial[:, half], late_clipped[1][:, half], 0.5, late_hi[:, half], ALU.mult, ALU.add)
-        for chunk, half in zip((2, 3), halves):
-            result = sbuf("result%d" % chunk, P)
-            nc.vector.scalar_tensor_tensor(result[:], late_clipped[2][:, half], 0.5, late_partial[:, half], ALU.mult, ALU.add)
+        both0 = sbuf("both0", 2 * P)
+        first12 = sbuf("first12", 2 * P)
+        gather(hi[:, targets(0, 2)], cen_t, 0, 2, bound_t[:, targets(0, 2)], ALU.add)
+        gather(hi[:, targets(2)], cen_t, 2, 1, bound_t[:, targets(2)], ALU.add)
+        gather(both0[:, targets(0)], pos1_t, 0, 1, hi[:, targets(0)], ALU.subtract)
+        gather(both0[:, targets(1)], pos2_t, 0, 1, hi[:, targets(0)], ALU.subtract)
+        for chunk in (1, 2):
+            gather(first12[:, targets(chunk - 1)], pos1_t, chunk, 1, hi[:, targets(chunk)], ALU.subtract)
+        totals = [open_total(chunk, hi[:, targets(chunk)], bank, total_bank)
+                  for chunk, bank, total_bank in ((0, "bank0", "bank6"), (1, "bank1", "bank7"), (2, "bank4", "bank0"))]
+        pull0 = relu("pull0", turned("both0_turned", "bank5", both0, 2)[:], 2 * P, scale=-0.5)
+        room0 = relu("room0", pull0[:], 2 * P, bias=b_col[:, 0:1], scale=-1.0)
+        for i in range(2):
+            turn(totals[0][:], room0[:, targets(i)], start=False, stop=i == 1)
+        pulls = [relu("pull%d" % chunk, turned("first_turned%d" % chunk, bank, first12[:, targets(chunk - 1)], 1)[:], P, scale=-0.5)
+                 for chunk, bank in ((1, "bank2"), (2, "bank3"))]
+        for chunk, pull in zip((1, 2), pulls):
+            add_room("room%d" % chunk, chunk, pull[:], totals[chunk], True)
+        store_total(0, totals[0])
+
+        second23 = sbuf("second23", 2 * P)
+        gather(hi[:, targets(3)], cen_t, 3, 1, bound_t[:, targets(3)], ALU.add)
+        gather(mixed[:, targets(0)], pos2_t, 1, 1, hi[:, targets(1)], ALU.subtract)
+        gather(mixed[:, targets(1)], pos1_t, 3, 1, hi[:, targets(3)], ALU.subtract)
+        gather(second23[:], pos2_t, 2, 2, hi[:, targets(2, 2)], ALU.subtract)
+        mixed_clipped = sbuf("mixed_clipped", 2 * P)
+        clipped23 = sbuf("clipped23", 2 * P)
+        partial3 = sbuf("partial3", P)
+        odd_floors = floor[:].rearrange("p (a c v) -> p a c v", a=2, c=2)[:, :, 1, :]
+        fused(mixed_clipped[:].rearrange("p (a v) -> p a v", a=2), mixed[:].rearrange("p (a v) -> p a v", a=2), 0.0, odd_floors, ALU.min, ALU.max)
+        fused(clipped23[:], second23[:], 0.0, floor[:, targets(2, 2)], ALU.min, ALU.max)
+        fused(partial3[:], mixed_clipped[:, targets(1)], 0.5, hi[:, targets(3)], ALU.mult, ALU.add)
+        for chunk, clipped, rest in ((1, mixed_clipped[:, targets(0)], totals[1]), (2, clipped23[:, targets(0)], totals[2]), (3, clipped23[:, targets(1)], partial3)):
+            result = sbuf("result%d" % chunk, P, tag="room2" if chunk == 3 else None)
+            fused(result[:], clipped, 0.5, rest[:], ALU.mult, ALU.add)
             nc.sync.dma_start(out[:, targets(chunk)], result[:])

@@ -72,12 +72,9 @@ def tile_picked_huber_none_p_kernel(tc, x_words, x_scales, w1, bound, offs, cen,
 
         floor = sbuf("floor", V)
         nc.scalar.activation(floor[:, targets(1, 3)], bound_t[:, targets(1, 3)], ACT.Copy, scale=-2.0)
-        hi = sbuf("hi", V)
-        mixed = sbuf("mixed", 2 * P)
-        shift2 = sbuf("shift2", 1)
-        shift = [hi[:, 3 * P : 3 * P + 1], mixed[:, 0:1], shift2[:]]
-        for chunk, rooms in enumerate((2, 1, 1)):
-            nc.scalar.activation(shift[chunk], b_col[:, chunk : chunk + 1], ACT.Copy, scale=-1.0 * rooms)
+        shift = sbuf("shift", 3)
+        nc.scalar.activation(shift[:, 0:1], b_col[:, 0:1], ACT.Copy, scale=-2.0)
+        nc.scalar.activation(shift[:, 1:3], b_col[:, 1:3], ACT.Copy, scale=-1.0)
 
         for first, count in ((0, 640), (640, 384)):
             picked = sbuf("scales%d" % first, count, U8)
@@ -123,9 +120,9 @@ def tile_picked_huber_none_p_kernel(tc, x_words, x_scales, w1, bound, offs, cen,
                 turn(held[:, targets(i)], source[:, targets(i)])
             return held
 
-        def open_total(chunk, centres, bank, total_bank):
+        def open_total(chunk, centres, total_bank):
             base = sbuf("base%d" % chunk, P)
-            nc.scalar.activation(base[:], turned("hi_turned%d" % chunk, bank, centres, 1)[:], ACT.Identity, bias=shift[chunk])
+            nc.scalar.activation(base[:], centres, ACT.Identity, bias=shift[:, chunk : chunk + 1])
             total = psum.tile([P, P], F32, name="total%d" % chunk, tag=total_bank)
             turn(total[:], base[:], start=True, stop=False)
             return total
@@ -142,24 +139,25 @@ def tile_picked_huber_none_p_kernel(tc, x_words, x_scales, w1, bound, offs, cen,
         def fused(into, first, scalar, second, op0, op1):
             nc.vector.scalar_tensor_tensor(into, first, scalar, second, op0, op1)
 
-        both0 = sbuf("both0", 2 * P)
+        hi = sbuf("hi", V)
+        mixed = sbuf("mixed", 2 * P)
         first12 = sbuf("first12", 2 * P)
+        first0, second0 = hi[:, targets(3)], mixed[:, targets(0)]
         gather(hi[:, targets(0, 2)], cen_t, 0, 2, bound_t[:, targets(0, 2)], ALU.add)
         gather(hi[:, targets(2)], cen_t, 2, 1, bound_t[:, targets(2)], ALU.add)
-        gather(both0[:, targets(0)], pos1_t, 0, 1, hi[:, targets(0)], ALU.subtract)
-        gather(both0[:, targets(1)], pos2_t, 0, 1, hi[:, targets(0)], ALU.subtract)
+        gather(first0, pos1_t, 0, 1, hi[:, targets(0)], ALU.subtract)
+        gather(second0, pos2_t, 0, 1, hi[:, targets(0)], ALU.subtract)
         for chunk in (1, 2):
             gather(first12[:, targets(chunk - 1)], pos1_t, chunk, 1, hi[:, targets(chunk)], ALU.subtract)
-        totals = [open_total(chunk, hi[:, targets(chunk)], bank, total_bank)
-                  for chunk, bank, total_bank in ((0, "bank0", "bank6"), (1, "bank1", "bank7"), (2, "bank4", "bank0"))]
-        pull0 = relu("pull0", turned("both0_turned", "bank5", both0, 2)[:], 2 * P, scale=-0.5)
-        room0 = relu("room0", pull0[:], 2 * P, bias=b_col[:, 0:1], scale=-1.0)
-        for i in range(2):
-            turn(totals[0][:], room0[:, targets(i)], start=False, stop=i == 1)
-        pulls = [relu("pull%d" % chunk, turned("first_turned%d" % chunk, bank, first12[:, targets(chunk - 1)], 1)[:], P, scale=-0.5)
-                 for chunk, bank in ((1, "bank2"), (2, "bank3"))]
-        for chunk, pull in zip((1, 2), pulls):
-            add_room("room%d" % chunk, chunk, pull[:], totals[chunk], True)
+        hi_turned = turned("hi_turned", "bank0", hi, 3)
+        totals = [open_total(chunk, hi_turned[:, targets(chunk)], bank) for chunk, bank in enumerate(("bank6", "bank7", "bank4"))]
+        pairs = [(first0, 0, "bank5"), (second0, 0, "bank3"), (first12[:, targets(0)], 1, "bank2"), (first12[:, targets(1)], 2, "bank1")]
+        banks = [turned("diff_turned%d" % i, bank, diff, 1) for i, (diff, chunk, bank) in enumerate(pairs)]
+        pulls = [relu("pull0", banks[0][:], P, scale=-0.5)]
+        for i, (diff, chunk, bank) in enumerate(pairs):
+            if i + 1 < len(pairs):
+                pulls.append(relu("pull%d" % (i + 1), banks[i + 1][:], P, scale=-0.5))
+            add_room("room%d" % i, chunk, pulls[i][:], totals[chunk], i > 0)
         store_total(0, totals[0])
 
         second23 = sbuf("second23", 2 * P)
@@ -175,6 +173,6 @@ def tile_picked_huber_none_p_kernel(tc, x_words, x_scales, w1, bound, offs, cen,
         fused(clipped23[:], second23[:], 0.0, floor[:, targets(2, 2)], ALU.min, ALU.max)
         fused(partial3[:], mixed_clipped[:, targets(1)], 0.5, hi[:, targets(3)], ALU.mult, ALU.add)
         for chunk, clipped, rest in ((1, mixed_clipped[:, targets(0)], totals[1]), (2, clipped23[:, targets(0)], totals[2]), (3, clipped23[:, targets(1)], partial3)):
-            result = sbuf("result%d" % chunk, P, tag="room2" if chunk == 3 else None)
+            result = sbuf("result%d" % chunk, P, tag="room3" if chunk == 3 else None)
             fused(result[:], clipped, 0.5, rest[:], ALU.mult, ALU.add)
             nc.sync.dma_start(out[:, targets(chunk)], result[:])

@@ -56,12 +56,12 @@ def tile_picked_huber_none_p_kernel(tc, x_words, x_scales, w1, bound, offs, cen,
         make_identity(nc, identity[:])
         nc.sync.dma_start(scale_table[112:P, :].bitcast(I32), x_scales[0].bitcast(I32))
         nc.sync.dma_start(offs_t[:], offs)
-        nc.sync.dma_start(word_table[:].bitcast(I32), x_words[0].bitcast(I32))
-        nc.sync.dma_start(w_raw[:], w1.rearrange("(p t) n -> p t n", t=PACK))
-        nc.sync.dma_start(bound_t[:], bound)
         nc.sync.dma_start(cen_t[:], cen)
         nc.sync.dma_start(pos1_t[:], pos1)
         nc.sync.dma_start(pos2_t[:], pos2)
+        nc.sync.dma_start(word_table[:].bitcast(I32), x_words[0].bitcast(I32))
+        nc.sync.dma_start(w_raw[:], w1.rearrange("(p t) n -> p t n", t=PACK))
+        nc.sync.dma_start(bound_t[:], bound)
         with nc.allow_non_contiguous_dma(reason="one bound to a partition"):
             nc.sync.dma_start(b_col[:], bound[0, targets(0, 3)].rearrange("(c p) -> p c", p=P))
 

@@ -46,7 +46,7 @@ def tile_picked_huber_none_p_kernel(tc, x_words, x_scales, w1, bound, offs, cen,
         scale_table = sbuf("scale_table", T, U8)
         identity = sbuf("identity", P)
         word_table = sbuf("word_table", T, U16)
-        b_col = sbuf("b_col", 3)
+        b_col = sbuf("b_col", 4)
         w_raw = keep.tile([P, PACK, N], F32, name="w_raw", tag="w_raw", align_bytes=64)
         bound_t = sbuf("bound_t", V)
         plane = sbuf("plane", S, U8)
@@ -63,7 +63,7 @@ def tile_picked_huber_none_p_kernel(tc, x_words, x_scales, w1, bound, offs, cen,
         nc.sync.dma_start(w_raw[:], w1.rearrange("(p t) n -> p t n", t=PACK))
         nc.sync.dma_start(bound_t[:], bound)
         with nc.allow_non_contiguous_dma(reason="one bound to a partition"):
-            nc.sync.dma_start(b_col[:], bound[0, targets(0, 3)].rearrange("(c p) -> p c", p=P))
+            nc.sync.dma_start(b_col[:], bound[0, :].rearrange("(c p) -> p c", p=P))
 
         w_bf = keep.tile([P, N, PACK], BF16, name="w_bf", align_bytes=64)
         w_codes = sbuf("w_codes", N, U32)
@@ -71,10 +71,9 @@ def tile_picked_huber_none_p_kernel(tc, x_words, x_scales, w1, bound, offs, cen,
         nc.scalar.activation(w_bf[:], w_raw[:].rearrange("p t n -> p n t"), ACT.Copy)
 
         floor = sbuf("floor", V)
-        nc.scalar.activation(floor[:, targets(1, 3)], bound_t[:, targets(1, 3)], ACT.Copy, scale=-2.0)
-        shift = sbuf("shift", 3)
-        nc.scalar.activation(shift[:, 0:1], b_col[:, 0:1], ACT.Copy, scale=-2.0)
-        nc.scalar.activation(shift[:, 1:3], b_col[:, 1:3], ACT.Copy, scale=-1.0)
+        nc.scalar.activation(floor[:], bound_t[:], ACT.Copy, scale=-2.0)
+        shift = sbuf("shift", 4)
+        nc.scalar.activation(shift[:], b_col[:], ACT.Copy, scale=-1.0)
 
         for first, count in ((0, 640), (640, 384)):
             picked = sbuf("scales%d" % first, count, U8)
@@ -120,59 +119,40 @@ def tile_picked_huber_none_p_kernel(tc, x_words, x_scales, w1, bound, offs, cen,
                 turn(held[:, targets(i)], source[:, targets(i)])
             return held
 
-        def open_total(chunk, centres, total_bank):
-            base = sbuf("base%d" % chunk, P)
-            nc.scalar.activation(base[:], centres, ACT.Identity, bias=shift[:, chunk : chunk + 1])
-            total = psum.tile([P, P], F32, name="total%d" % chunk, tag=total_bank)
-            turn(total[:], base[:], start=True, stop=False)
-            return total
-
-        def add_room(name, chunk, pull, total, last):
-            room = relu(name, pull, P, bias=b_col[:, chunk : chunk + 1], scale=-1.0)
-            turn(total[:], room[:], start=False, stop=last)
-
-        def store_total(chunk, total):
-            result = sbuf("result%d" % chunk, P)
-            nc.scalar.activation(result[:], total[:], ACT.Copy)
-            nc.sync.dma_start(out[:, targets(chunk)], result[:])
-
         def fused(into, first, scalar, second, op0, op1):
             nc.vector.scalar_tensor_tensor(into, first, scalar, second, op0, op1)
 
         hi = sbuf("hi", V)
-        mixed = sbuf("mixed", 2 * P)
-        first12 = sbuf("first12", 2 * P)
-        first0, second0 = hi[:, targets(3)], mixed[:, targets(0)]
-        gather(hi[:, targets(0, 2)], cen_t, 0, 2, bound_t[:, targets(0, 2)], ALU.add)
-        gather(hi[:, targets(2)], cen_t, 2, 1, bound_t[:, targets(2)], ALU.add)
-        gather(first0, pos1_t, 0, 1, hi[:, targets(0)], ALU.subtract)
-        gather(second0, pos2_t, 0, 1, hi[:, targets(0)], ALU.subtract)
-        for chunk in (1, 2):
-            gather(first12[:, targets(chunk - 1)], pos1_t, chunk, 1, hi[:, targets(chunk)], ALU.subtract)
-        hi_turned = turned("hi_turned", "bank0", hi, 3)
-        totals = [open_total(chunk, hi_turned[:, targets(chunk)], bank) for chunk, bank in enumerate(("bank6", "bank7", "bank4"))]
-        pairs = [(first0, 0, "bank5"), (second0, 0, "bank3"), (first12[:, targets(0)], 1, "bank2"), (first12[:, targets(1)], 2, "bank1")]
-        banks = [turned("diff_turned%d" % i, bank, diff, 1) for i, (diff, chunk, bank) in enumerate(pairs)]
-        pulls = [relu("pull0", banks[0][:], P, scale=-0.5)]
-        for i, (diff, chunk, bank) in enumerate(pairs):
-            if i + 1 < len(pairs):
-                pulls.append(relu("pull%d" % (i + 1), banks[i + 1][:], P, scale=-0.5))
-            add_room("room%d" % i, chunk, pulls[i][:], totals[chunk], i > 0)
-        store_total(0, totals[0])
+        first = sbuf("first", V)
+        second = sbuf("second", V)
+        for chunk in (0, 2):
+            gather(hi[:, targets(chunk, 2)], cen_t, chunk, 2, bound_t[:, targets(chunk, 2)], ALU.add)
+        for chunk, chunks in ((0, 2), (2, 1), (3, 1)):
+            gather(first[:, targets(chunk, chunks)], pos1_t, chunk, chunks, hi[:, targets(chunk, chunks)], ALU.subtract)
+        for chunk in (0, 2):
+            gather(second[:, targets(chunk, 2)], pos2_t, chunk, 2, hi[:, targets(chunk, 2)], ALU.subtract)
 
-        second23 = sbuf("second23", 2 * P)
-        gather(hi[:, targets(3)], cen_t, 3, 1, bound_t[:, targets(3)], ALU.add)
-        gather(mixed[:, targets(0)], pos2_t, 1, 1, hi[:, targets(1)], ALU.subtract)
-        gather(mixed[:, targets(1)], pos1_t, 3, 1, hi[:, targets(3)], ALU.subtract)
-        gather(second23[:], pos2_t, 2, 2, hi[:, targets(2, 2)], ALU.subtract)
-        mixed_clipped = sbuf("mixed_clipped", 2 * P)
-        clipped23 = sbuf("clipped23", 2 * P)
-        partial3 = sbuf("partial3", P)
-        odd_floors = floor[:].rearrange("p (a c v) -> p a c v", a=2, c=2)[:, :, 1, :]
-        fused(mixed_clipped[:].rearrange("p (a v) -> p a v", a=2), mixed[:].rearrange("p (a v) -> p a v", a=2), 0.0, odd_floors, ALU.min, ALU.max)
-        fused(clipped23[:], second23[:], 0.0, floor[:, targets(2, 2)], ALU.min, ALU.max)
-        fused(partial3[:], mixed_clipped[:, targets(1)], 0.5, hi[:, targets(3)], ALU.mult, ALU.add)
-        for chunk, clipped, rest in ((1, mixed_clipped[:, targets(0)], totals[1]), (2, clipped23[:, targets(0)], totals[2]), (3, clipped23[:, targets(1)], partial3)):
-            result = sbuf("result%d" % chunk, P, tag="room3" if chunk == 3 else None)
-            fused(result[:], clipped, 0.5, rest[:], ALU.mult, ALU.add)
+        bases = []
+        for chunk in (0, 2):
+            hi_turned = turned("hi_turned%d" % chunk, "bank%d" % (6 + chunk // 2), hi[:, targets(chunk, 2)], 2)
+            for i in range(2):
+                bases.append(sbuf("base%d" % (chunk + i), P))
+                nc.scalar.activation(bases[chunk + i][:], hi_turned[:, targets(i)], ACT.Identity, bias=shift[:, chunk + i : chunk + i + 1])
+        first_turned = [turned("first_turned%d" % chunk, "bank%d" % chunk, first[:, targets(chunk)], 1) for chunk in range(4)]
+        pulls = [relu("pull0", first_turned[0][:], P, scale=-0.5)]
+        totals = []
+        for chunk in range(4):
+            if chunk < 3:
+                pulls.append(relu("pull%d" % (chunk + 1), first_turned[chunk + 1][:], P, scale=-0.5))
+            totals.append(psum.tile([P, P], F32, name="total%d" % chunk, tag="bank%d" % chunk))
+            turn(totals[chunk][:], bases[chunk][:], start=True, stop=False)
+            room = relu("room%d" % chunk, pulls[chunk][:], P, bias=b_col[:, chunk : chunk + 1], scale=-1.0)
+            turn(totals[chunk][:], room[:], start=False, stop=True)
+
+        clipped = sbuf("clipped", V)
+        for chunk in (0, 2):
+            fused(clipped[:, targets(chunk, 2)], second[:, targets(chunk, 2)], 0.0, floor[:, targets(chunk, 2)], ALU.min, ALU.max)
+        for chunk in range(4):
+            result = sbuf("result%d" % chunk, P)
+            fused(result[:], clipped[:, targets(chunk)], 0.5, totals[chunk][:], ALU.mult, ALU.add)
             nc.sync.dma_start(out[:, targets(chunk)], result[:])

@@ -46,9 +46,9 @@ def tile_picked_huber_none_p_kernel(tc, x_words, x_scales, w1, bound, offs, cen,
         scale_table = sbuf("scale_table", T, U8)
         identity = sbuf("identity", P)
         word_table = sbuf("word_table", T, U16)
-        b_col = sbuf("b_col", 4)
+        b_col = sbuf("b_col", 3)
         w_raw = keep.tile([P, PACK, N], F32, name="w_raw", tag="w_raw", align_bytes=64)
-        bound_t = sbuf("bound_t", V)
+        bound_t = sbuf("bound_t", P)
         plane = sbuf("plane", S, U8)
 
         nc.vector.memset(scale_table[0:112, :].bitcast(I32), 0)
@@ -61,18 +61,20 @@ def tile_picked_huber_none_p_kernel(tc, x_words, x_scales, w1, bound, offs, cen,
         nc.sync.dma_start(pos2_t[:], pos2)
         nc.sync.dma_start(word_table[:].bitcast(I32), x_words[0].bitcast(I32))
         nc.sync.dma_start(w_raw[:], w1.rearrange("(p t) n -> p t n", t=PACK))
-        nc.sync.dma_start(bound_t[:], bound)
+        nc.sync.dma_start(bound_t[:], bound[:, targets(3)])
         with nc.allow_non_contiguous_dma(reason="one bound to a partition"):
-            nc.sync.dma_start(b_col[:], bound[0, :].rearrange("(c p) -> p c", p=P))
+            nc.sync.dma_start(b_col[:], bound[0, 0 : 3 * P].rearrange("(c p) -> p c", p=P))
 
         w_bf = keep.tile([P, N, PACK], BF16, name="w_bf", align_bytes=64)
         w_codes = sbuf("w_codes", N, U32)
         w_scales = sbuf("w_scales", N, U8)
         nc.scalar.activation(w_bf[:], w_raw[:].rearrange("p t n -> p n t"), ACT.Copy)
 
-        floor = sbuf("floor", V)
+        floor = sbuf("floor", P)
         nc.scalar.activation(floor[:], bound_t[:], ACT.Copy, scale=-2.0)
-        shift = sbuf("shift", 4)
+        minus_one = sbuf("minus_one", P)
+        nc.gpsimd.memset(minus_one[:], -1.0)
+        shift = sbuf("shift", 3)
         nc.scalar.activation(shift[:], b_col[:], ACT.Copy, scale=-1.0)
 
         for first, count in ((0, 640), (640, 384)):
@@ -105,54 +107,80 @@ def tile_picked_huber_none_p_kernel(tc, x_words, x_scales, w1, bound, offs, cen,
         def turn(bank, source, start=True, stop=True):
             nc.tensor.matmul(bank, source, identity[:], start=start, stop=stop, is_transpose=True)
 
-        def gather(into, list_tile, chunk, chunks, other, op):
-            nc.vector.tensor_tensor(into, y[:].indirect(entries(list_tile, chunk * P, chunks * P)), other, op)
+        def picked_from_y(list_tile, chunk):
+            return y[:].indirect(entries(list_tile, chunk * P, P))
 
-        def relu(name, source, columns, **affine):
-            made = sbuf(name, columns)
-            nc.scalar.activation(made[:], source, ACT.Relu, **affine)
+        def scalar_gather(name, list_tile, chunk, scale=1.0):
+            made = sbuf(name, P)
+            nc.scalar.activation(made[:], picked_from_y(list_tile, chunk), ACT.Copy, scale=scale)
             return made
 
-        def turned(name, bank, source, chunks):
-            held = psum.tile([P, chunks * P], F32, name=name, tag=bank)
-            for i in range(chunks):
-                turn(held[:, targets(i)], source[:, targets(i)])
-            return held
+        def vector_gather(name, list_tile, chunk):
+            made = sbuf(name, P)
+            nc.vector.tensor_copy(made[:], picked_from_y(list_tile, chunk))
+            return made
 
         def fused(into, first, scalar, second, op0, op1):
             nc.vector.scalar_tensor_tensor(into, first, scalar, second, op0, op1)
 
-        hi = sbuf("hi", V)
-        first = sbuf("first", V)
-        second = sbuf("second", V)
-        for chunk in (0, 2):
-            gather(hi[:, targets(chunk, 2)], cen_t, chunk, 2, bound_t[:, targets(chunk, 2)], ALU.add)
-        for chunk, chunks in ((0, 2), (2, 1), (3, 1)):
-            gather(first[:, targets(chunk, chunks)], pos1_t, chunk, chunks, hi[:, targets(chunk, chunks)], ALU.subtract)
-        for chunk in (0, 2):
-            gather(second[:, targets(chunk, 2)], pos2_t, chunk, 2, hi[:, targets(chunk, 2)], ALU.subtract)
+        def vector_fused(name, list_tile, chunk, other, op, tag=None):
+            made = sbuf(name, P, tag=tag)
+            nc.vector.tensor_tensor(made[:], picked_from_y(list_tile, chunk), other[:], op)
+            return made
 
-        bases = []
-        for chunk in (0, 2):
-            hi_turned = turned("hi_turned%d" % chunk, "bank%d" % (6 + chunk // 2), hi[:, targets(chunk, 2)], 2)
-            for i in range(2):
-                bases.append(sbuf("base%d" % (chunk + i), P))
-                nc.scalar.activation(bases[chunk + i][:], hi_turned[:, targets(i)], ACT.Identity, bias=shift[:, chunk + i : chunk + i + 1])
-        first_turned = [turned("first_turned%d" % chunk, "bank%d" % chunk, first[:, targets(chunk)], 1) for chunk in range(4)]
-        pulls = [relu("pull0", first_turned[0][:], P, scale=-0.5)]
-        totals = []
-        for chunk in range(4):
-            if chunk < 3:
-                pulls.append(relu("pull%d" % (chunk + 1), first_turned[chunk + 1][:], P, scale=-0.5))
-            totals.append(psum.tile([P, P], F32, name="total%d" % chunk, tag="bank%d" % chunk))
-            turn(totals[chunk][:], bases[chunk][:], start=True, stop=False)
-            room = relu("room%d" % chunk, pulls[chunk][:], P, bias=b_col[:, chunk : chunk + 1], scale=-1.0)
-            turn(totals[chunk][:], room[:], start=False, stop=True)
+        minus_centre = [None] * 3
+        minus_centre[1] = vector_fused("mc1", cen_t, 1, minus_one, ALU.mult)
+        minus_centre[0] = scalar_gather("mc0", cen_t, 0, -1.0)
+        hi = vector_fused("hi", cen_t, 3, bound_t, ALU.add)
+        first0 = scalar_gather("first0", pos1_t, 0)
+        diff_second0 = vector_fused("diff_second0", pos2_t, 0, minus_centre[0], ALU.add)
+        diff_first1 = vector_fused("diff_first1", pos1_t, 1, minus_centre[1], ALU.add)
+        minus_centre[2] = scalar_gather("mc2", cen_t, 2, -1.0)
+        diff_second1 = vector_fused("diff_second1", pos2_t, 1, minus_centre[1], ALU.add)
+        first2 = scalar_gather("first2", pos1_t, 2)
+        second2 = scalar_gather("second2", pos2_t, 2)
+        terms = (((minus_centre[0], first0), (diff_second0,)),
+                 ((diff_first1,), (diff_second1,)),
+                 ((minus_centre[2], first2), (minus_centre[2], second2)))
 
-        clipped = sbuf("clipped", V)
-        for chunk in (0, 2):
-            fused(clipped[:, targets(chunk, 2)], second[:, targets(chunk, 2)], 0.0, floor[:, targets(chunk, 2)], ALU.min, ALU.max)
-        for chunk in range(4):
-            result = sbuf("result%d" % chunk, P)
-            fused(result[:], clipped[:, targets(chunk)], 0.5, totals[chunk][:], ALU.mult, ALU.add)
-            nc.sync.dma_start(out[:, targets(chunk)], result[:])
+        diffs = []
+        for chunk in range(3):
+            diffs.append(psum.tile([P, 2 * P], F32, name="diffs%d" % chunk, tag="bank%d" % chunk))
+            for i, summands in enumerate(terms[chunk]):
+                for place, summand in enumerate(summands):
+                    turn(diffs[chunk][:, targets(i)], summand[:], start=place == 0, stop=place == len(summands) - 1)
+        below_first = sbuf("below_first", P)
+        nc.vector.tensor_tensor(below_first[:], picked_from_y(pos1_t, 3), hi[:], ALU.subtract)
+        second3 = scalar_gather("second3", pos2_t, 3)
+
+        totals, clips = [], []
+        for chunk in range(3):
+            clips.append(sbuf("clips%d" % chunk, 2 * P))
+            nc.vector.tensor_scalar(clips[chunk][:], diffs[chunk][:], b_col[:, chunk : chunk + 1], shift[:, chunk : chunk + 1], ALU.min, ALU.max)
+            if chunk == 0:
+                clipped_first = sbuf("clipped_first", P, tag="diff_second0")
+                fused(clipped_first[:], below_first[:], 0.0, floor[:], ALU.min, ALU.max)
+            if chunk == 1:
+                below_second = sbuf("below_second", P, tag="diff_second1")
+                nc.vector.tensor_tensor(below_second[:], second3[:], hi[:], ALU.subtract)
+        for chunk, bank in enumerate(("bank1", "bank3", "bank4")):
+            totals.append(psum.tile([P, P], F32, name="total%d" % chunk, tag=bank))
+            turn(totals[chunk][:], clips[chunk][:, targets(0)], start=True, stop=False)
+            turn(totals[chunk][:], clips[chunk][:, targets(1)], start=False, stop=True)
+
+        late = sbuf("late", 3 * P, tag="second2")
+
+        def finish(chunk, result):
+            fused(result, totals[chunk][:], 0.5, minus_centre[chunk][:], ALU.mult, ALU.subtract)
+            nc.sync.dma_start(out[:, targets(chunk)], result)
+
+        clipped_second = late[:, targets(2)]
+        fused(clipped_second, below_second[:], 0.0, floor[:], ALU.min, ALU.max)
+        finish(0, late[:, targets(0)])
+        partial = sbuf("partial", P, tag="clips0")
+        fused(partial[:], clipped_first[:], 0.5, hi[:], ALU.mult, ALU.add)
+        finish(1, late[:, targets(1)])
+        last = sbuf("last", P, tag="clips1")
+        fused(last[:], clipped_second, 0.5, partial[:], ALU.mult, ALU.add)
+        nc.sync.dma_start(out[:, targets(3)], last[:])
+        finish(2, sbuf("result2", P)[:])

@@ -48,7 +48,7 @@ def tile_picked_huber_none_p_kernel(tc, x_words, x_scales, w1, bound, offs, cen,
         word_table = sbuf("word_table", T, U16)
         b_col = sbuf("b_col", 3)
         w_raw = keep.tile([P, PACK, N], F32, name="w_raw", tag="w_raw", align_bytes=64)
-        bound_t = sbuf("bound_t", P)
+        bound_t = sbuf("bound_t", 2 * P)
         plane = sbuf("plane", S, U8)
 
         nc.vector.memset(scale_table[0:112, :].bitcast(I32), 0)
@@ -61,7 +61,7 @@ def tile_picked_huber_none_p_kernel(tc, x_words, x_scales, w1, bound, offs, cen,
         nc.sync.dma_start(pos2_t[:], pos2)
         nc.sync.dma_start(word_table[:].bitcast(I32), x_words[0].bitcast(I32))
         nc.sync.dma_start(w_raw[:], w1.rearrange("(p t) n -> p t n", t=PACK))
-        nc.sync.dma_start(bound_t[:], bound[:, targets(3)])
+        nc.sync.dma_start(bound_t[:], bound[:, targets(2, 2)])
         with nc.allow_non_contiguous_dma(reason="one bound to a partition"):
             nc.sync.dma_start(b_col[:], bound[0, 0 : 3 * P].rearrange("(c p) -> p c", p=P))
 
@@ -70,12 +70,15 @@ def tile_picked_huber_none_p_kernel(tc, x_words, x_scales, w1, bound, offs, cen,
         w_scales = sbuf("w_scales", N, U8)
         nc.scalar.activation(w_bf[:], w_raw[:].rearrange("p t n -> p n t"), ACT.Copy)
 
-        floor = sbuf("floor", P)
-        nc.scalar.activation(floor[:], bound_t[:], ACT.Copy, scale=-2.0)
-        minus_one = sbuf("minus_one", P)
-        nc.gpsimd.memset(minus_one[:], -1.0)
-        shift = sbuf("shift", 3)
-        nc.scalar.activation(shift[:], b_col[:], ACT.Copy, scale=-1.0)
+        floor = sbuf("floor", 2 * P)
+        for i in range(2):
+            nc.scalar.activation(floor[:, targets(i)], bound_t[:, targets(1)], ACT.Copy, scale=-2.0)
+        minus_b = sbuf("minus_b", 2)
+        nc.scalar.activation(minus_b[:], b_col[:, 0:2], ACT.Copy, scale=-1.0)
+        half_b = sbuf("half_b", 1)
+        nc.scalar.activation(half_b[:], b_col[:, 0:1], ACT.Copy, scale=0.5)
+        floor_col = sbuf("floor_col", 1)
+        nc.scalar.activation(floor_col[:], b_col[:, 2:3], ACT.Copy, scale=-2.0)
 
         for first, count in ((0, 640), (640, 384)):
             picked = sbuf("scales%d" % first, count, U8)
@@ -107,80 +110,73 @@ def tile_picked_huber_none_p_kernel(tc, x_words, x_scales, w1, bound, offs, cen,
         def turn(bank, source, start=True, stop=True):
             nc.tensor.matmul(bank, source, identity[:], start=start, stop=stop, is_transpose=True)
 
-        def picked_from_y(list_tile, chunk):
-            return y[:].indirect(entries(list_tile, chunk * P, P))
+        def picked_from_y(list_tile, chunk, chunks=1):
+            return y[:].indirect(entries(list_tile, chunk * P, chunks * P))
 
         def scalar_gather(name, list_tile, chunk, scale=1.0):
             made = sbuf(name, P)
             nc.scalar.activation(made[:], picked_from_y(list_tile, chunk), ACT.Copy, scale=scale)
             return made
 
-        def vector_gather(name, list_tile, chunk):
-            made = sbuf(name, P)
-            nc.vector.tensor_copy(made[:], picked_from_y(list_tile, chunk))
-            return made
+        def vector_gather(into, list_tile, chunk, chunks, other, op):
+            nc.vector.tensor_tensor(into, picked_from_y(list_tile, chunk, chunks), other, op)
 
         def fused(into, first, scalar, second, op0, op1):
             nc.vector.scalar_tensor_tensor(into, first, scalar, second, op0, op1)
 
-        def vector_fused(name, list_tile, chunk, other, op, tag=None):
-            made = sbuf(name, P, tag=tag)
-            nc.vector.tensor_tensor(made[:], picked_from_y(list_tile, chunk), other[:], op)
-            return made
-
-        minus_centre = [None] * 3
-        minus_centre[1] = vector_fused("mc1", cen_t, 1, minus_one, ALU.mult)
-        minus_centre[0] = scalar_gather("mc0", cen_t, 0, -1.0)
-        hi = vector_fused("hi", cen_t, 3, bound_t, ALU.add)
+        hi = sbuf("hi", 2 * P)
+        vector_gather(hi[:], cen_t, 2, 2, bound_t[:], ALU.add)
+        minus_centre0 = scalar_gather("minus_centre0", cen_t, 0, -1.0)
+        minus_centre1 = scalar_gather("minus_centre1", cen_t, 1, -1.0)
         first0 = scalar_gather("first0", pos1_t, 0)
-        diff_second0 = vector_fused("diff_second0", pos2_t, 0, minus_centre[0], ALU.add)
-        diff_first1 = vector_fused("diff_first1", pos1_t, 1, minus_centre[1], ALU.add)
-        minus_centre[2] = scalar_gather("mc2", cen_t, 2, -1.0)
-        diff_second1 = vector_fused("diff_second1", pos2_t, 1, minus_centre[1], ALU.add)
-        first2 = scalar_gather("first2", pos1_t, 2)
-        second2 = scalar_gather("second2", pos2_t, 2)
-        terms = (((minus_centre[0], first0), (diff_second0,)),
-                 ((diff_first1,), (diff_second1,)),
-                 ((minus_centre[2], first2), (minus_centre[2], second2)))
+        first1 = scalar_gather("first1", pos1_t, 1)
+        second1 = scalar_gather("second1", pos2_t, 1)
+        diff0 = sbuf("diff0", P)
+        vector_gather(diff0[:], pos2_t, 0, 1, minus_centre0[:], ALU.add)
+        below = {}
+        for chunk in (2, 3):
+            below[chunk] = sbuf("below%d" % chunk, 2 * P)
+            for i, list_tile in enumerate((pos1_t, pos2_t)):
+                vector_gather(below[chunk][:, targets(i)], list_tile, chunk, 1, hi[:, targets(chunk - 2)], ALU.subtract)
 
-        diffs = []
-        for chunk in range(3):
-            diffs.append(psum.tile([P, 2 * P], F32, name="diffs%d" % chunk, tag="bank%d" % chunk))
-            for i, summands in enumerate(terms[chunk]):
-                for place, summand in enumerate(summands):
-                    turn(diffs[chunk][:, targets(i)], summand[:], start=place == 0, stop=place == len(summands) - 1)
-        below_first = sbuf("below_first", P)
-        nc.vector.tensor_tensor(below_first[:], picked_from_y(pos1_t, 3), hi[:], ALU.subtract)
-        second3 = scalar_gather("second3", pos2_t, 3)
+        def turned(name, bank, *summands):
+            held = psum.tile([P, P], F32, name=name, tag=bank)
+            for place, summand in enumerate(summands):
+                turn(held[:], summand[:], start=place == 0, stop=place == len(summands) - 1)
+            return held
 
-        totals, clips = [], []
-        for chunk in range(3):
-            clips.append(sbuf("clips%d" % chunk, 2 * P))
-            nc.vector.tensor_scalar(clips[chunk][:], diffs[chunk][:], b_col[:, chunk : chunk + 1], shift[:, chunk : chunk + 1], ALU.min, ALU.max)
+        diffs0 = (turned("diff_first0", "bank0", minus_centre0, first0), turned("diff_second0", "bank5", diff0))
+        diffs1 = (turned("diff_first1", "bank1", minus_centre1, first1), turned("diff_second1", "bank7", minus_centre1, second1))
+        diffs2 = psum.tile([P, 2 * P], F32, name="diffs2", tag="bank4")
+        for i in range(2):
+            turn(diffs2[:, targets(i)], below[2][:, targets(i)])
+
+        clips = [sbuf("clips%d" % chunk, 2 * P) for chunk in range(3)]
+        lifted = sbuf("lifted", 2 * P)
+        for i in range(2):
+            nc.scalar.activation(lifted[:, targets(i)], diffs0[i][:], ACT.Relu, bias=half_b[:], scale=0.5)
+        for i in range(2):
+            nc.scalar.activation(clips[0][:, targets(i)], lifted[:, targets(i)], ACT.Relu, bias=b_col[:, 0:1], scale=-1.0)
+        for i in range(2):
+            nc.vector.tensor_scalar(clips[1][:, targets(i)], diffs1[i][:], b_col[:, 1:2], minus_b[:, 1:2], ALU.min, ALU.max)
+        nc.vector.tensor_scalar(clips[2][:], diffs2[:], 0.0, floor_col[:], ALU.min, ALU.max)
+        clipped = below[2]
+        fused(clipped[:], below[3][:], 0.0, floor[:], ALU.min, ALU.max)
+        totals = {}
+        for chunk, bank in ((1, "bank3"), (0, "bank6"), (2, "bank2")):
+            totals[chunk] = psum.tile([P, P], F32, name="total%d" % chunk, tag=bank)
             if chunk == 0:
-                clipped_first = sbuf("clipped_first", P, tag="diff_second0")
-                fused(clipped_first[:], below_first[:], 0.0, floor[:], ALU.min, ALU.max)
-            if chunk == 1:
-                below_second = sbuf("below_second", P, tag="diff_second1")
-                nc.vector.tensor_tensor(below_second[:], second3[:], hi[:], ALU.subtract)
-        for chunk, bank in enumerate(("bank1", "bank3", "bank4")):
-            totals.append(psum.tile([P, P], F32, name="total%d" % chunk, tag=bank))
-            turn(totals[chunk][:], clips[chunk][:, targets(0)], start=True, stop=False)
+                turn(totals[chunk][:], minus_b[:, 0:1].to_broadcast([P, P]), start=True, stop=False)
+            turn(totals[chunk][:], clips[chunk][:, targets(0)], start=chunk != 0, stop=False)
             turn(totals[chunk][:], clips[chunk][:, targets(1)], start=False, stop=True)
 
-        late = sbuf("late", 3 * P, tag="second2")
-
-        def finish(chunk, result):
-            fused(result, totals[chunk][:], 0.5, minus_centre[chunk][:], ALU.mult, ALU.subtract)
+        def finish(chunk, result, first, scalar, second, op):
+            fused(result, first, scalar, second, ALU.mult, op)
             nc.sync.dma_start(out[:, targets(chunk)], result)
 
-        clipped_second = late[:, targets(2)]
-        fused(clipped_second, below_second[:], 0.0, floor[:], ALU.min, ALU.max)
-        finish(0, late[:, targets(0)])
-        partial = sbuf("partial", P, tag="clips0")
-        fused(partial[:], clipped_first[:], 0.5, hi[:], ALU.mult, ALU.add)
-        finish(1, late[:, targets(1)])
-        last = sbuf("last", P, tag="clips1")
-        fused(last[:], clipped_second, 0.5, partial[:], ALU.mult, ALU.add)
-        nc.sync.dma_start(out[:, targets(3)], last[:])
-        finish(2, sbuf("result2", P)[:])
+        finish(1, sbuf("result1", P)[:], totals[1][:], 0.5, minus_centre1[:], ALU.subtract)
+        partial = clips[1][:, targets(1)]
+        fused(partial, clipped[:, targets(0)], 0.5, hi[:, targets(1)], ALU.mult, ALU.add)
+        finish(0, sbuf("result0", P)[:], totals[0][:], -1.0, minus_centre0[:], ALU.subtract)
+        finish(3, clips[0][:, targets(1)], clipped[:, targets(1)], 0.5, partial, ALU.add)
+        finish(2, sbuf("result2", P)[:], totals[2][:], 0.5, hi[:, targets(0)], ALU.add)

@@ -71,12 +71,13 @@ def tile_picked_huber_none_p_kernel(tc, x_words, x_scales, w1, bound, offs, cen,
         nc.scalar.activation(w_bf[:], w_raw[:].rearrange("p t n -> p n t"), ACT.Copy)
 
         floor = sbuf("floor", 2 * P)
-        for i in range(2):
-            nc.scalar.activation(floor[:, targets(i)], bound_t[:, targets(1)], ACT.Copy, scale=-2.0)
+        nc.scalar.activation(floor[:], bound_t[:], ACT.Copy, scale=-2.0)
         minus_b = sbuf("minus_b", 2)
         nc.scalar.activation(minus_b[:], b_col[:, 0:2], ACT.Copy, scale=-1.0)
         half_b = sbuf("half_b", 1)
         nc.scalar.activation(half_b[:], b_col[:, 0:1], ACT.Copy, scale=0.5)
+        two_b = sbuf("two_b", 1)
+        nc.scalar.activation(two_b[:], b_col[:, 1:2], ACT.Copy, scale=2.0)
         floor_col = sbuf("floor_col", 1)
         nc.scalar.activation(floor_col[:], b_col[:, 2:3], ACT.Copy, scale=-2.0)
 
@@ -133,11 +134,10 @@ def tile_picked_huber_none_p_kernel(tc, x_words, x_scales, w1, bound, offs, cen,
         second1 = scalar_gather("second1", pos2_t, 1)
         diff0 = sbuf("diff0", P)
         vector_gather(diff0[:], pos2_t, 0, 1, minus_centre0[:], ALU.add)
-        below = {}
-        for chunk in (2, 3):
-            below[chunk] = sbuf("below%d" % chunk, 2 * P)
-            for i, list_tile in enumerate((pos1_t, pos2_t)):
-                vector_gather(below[chunk][:, targets(i)], list_tile, chunk, 1, hi[:, targets(chunk - 2)], ALU.subtract)
+        below_first = sbuf("below_first", 2 * P)
+        vector_gather(below_first[:], pos1_t, 2, 2, hi[:], ALU.subtract)
+        below_second = sbuf("below_second", 2 * P)
+        vector_gather(below_second[:], pos2_t, 2, 2, hi[:], ALU.subtract)
 
         def turned(name, bank, *summands):
             held = psum.tile([P, P], F32, name=name, tag=bank)
@@ -147,36 +147,39 @@ def tile_picked_huber_none_p_kernel(tc, x_words, x_scales, w1, bound, offs, cen,
 
         diffs0 = (turned("diff_first0", "bank0", minus_centre0, first0), turned("diff_second0", "bank5", diff0))
         diffs1 = (turned("diff_first1", "bank1", minus_centre1, first1), turned("diff_second1", "bank7", minus_centre1, second1))
-        diffs2 = psum.tile([P, 2 * P], F32, name="diffs2", tag="bank4")
-        for i in range(2):
-            turn(diffs2[:, targets(i)], below[2][:, targets(i)])
+        diff2 = turned("diff_first2", "bank4", below_first[:, targets(0)])
 
-        clips = [sbuf("clips%d" % chunk, 2 * P) for chunk in range(3)]
-        lifted = sbuf("lifted", 2 * P)
-        for i in range(2):
-            nc.scalar.activation(lifted[:, targets(i)], diffs0[i][:], ACT.Relu, bias=half_b[:], scale=0.5)
-        for i in range(2):
-            nc.scalar.activation(clips[0][:, targets(i)], lifted[:, targets(i)], ACT.Relu, bias=b_col[:, 0:1], scale=-1.0)
-        for i in range(2):
-            nc.vector.tensor_scalar(clips[1][:, targets(i)], diffs1[i][:], b_col[:, 1:2], minus_b[:, 1:2], ALU.min, ALU.max)
-        nc.vector.tensor_scalar(clips[2][:], diffs2[:], 0.0, floor_col[:], ALU.min, ALU.max)
-        clipped = below[2]
-        fused(clipped[:], below[3][:], 0.0, floor[:], ALU.min, ALU.max)
-        totals = {}
-        for chunk, bank in ((1, "bank3"), (0, "bank6"), (2, "bank2")):
-            totals[chunk] = psum.tile([P, P], F32, name="total%d" % chunk, tag=bank)
-            if chunk == 0:
-                turn(totals[chunk][:], minus_b[:, 0:1].to_broadcast([P, P]), start=True, stop=False)
-            turn(totals[chunk][:], clips[chunk][:, targets(0)], start=chunk != 0, stop=False)
-            turn(totals[chunk][:], clips[chunk][:, targets(1)], start=False, stop=True)
+        def relu(name, source, bias, scale):
+            made = sbuf(name, P)
+            nc.scalar.activation(made[:], source[:], ACT.Relu, bias=bias, scale=scale)
+            return made
 
-        def finish(chunk, result, first, scalar, second, op):
-            fused(result, first, scalar, second, ALU.mult, op)
-            nc.sync.dma_start(out[:, targets(chunk)], result)
+        lifted = [relu("lifted%d" % i, diffs0[i], half_b[:], 0.5) for i in range(2)]
+        lifted.append(relu("lifted2", diffs1[0], b_col[:, 1:2], -1.0))
+        rooms = [relu("room%d" % i, lifted[i], b_col[:, 0:1], -1.0) for i in range(2)]
+        rooms.append(relu("room2", lifted[2], two_b[:], -1.0))
 
-        finish(1, sbuf("result1", P)[:], totals[1][:], 0.5, minus_centre1[:], ALU.subtract)
-        partial = clips[1][:, targets(1)]
-        fused(partial, clipped[:, targets(0)], 0.5, hi[:, targets(1)], ALU.mult, ALU.add)
-        finish(0, sbuf("result0", P)[:], totals[0][:], -1.0, minus_centre0[:], ALU.subtract)
-        finish(3, clips[0][:, targets(1)], clipped[:, targets(1)], 0.5, partial, ALU.add)
-        finish(2, sbuf("result2", P)[:], totals[2][:], 0.5, hi[:, targets(0)], ALU.add)
+        clipped_first = sbuf("clipped_first", P)
+        fused(clipped_first[:], below_first[:, targets(1)], 0.0, floor[:, targets(1)], ALU.min, ALU.max)
+        clipped_second = sbuf("clipped_second", 2 * P)
+        fused(clipped_second[:], below_second[:], 0.0, floor[:], ALU.min, ALU.max)
+        clip1 = below_first[:, targets(1)]
+        nc.vector.tensor_scalar(clip1, diffs1[1][:], b_col[:, 1:2], minus_b[:, 1:2], ALU.min, ALU.max)
+        clip2 = sbuf("clip2", P)
+        nc.vector.tensor_scalar(clip2[:], diff2[:], 0.0, floor_col[:], ALU.min, ALU.max)
+        total0 = turned("total0", "bank6", minus_b[:, 0:1].to_broadcast([P, P]), rooms[0], rooms[1])
+        total1 = turned("total1", "bank3", minus_b[:, 1:2].to_broadcast([P, P]), clip1, rooms[2])
+        total2 = turned("total2", "bank2", clip2)
+
+        def finish(chunk, first, scalar, second, op):
+            result = sbuf("result%d" % chunk, P)
+            fused(result[:], first, scalar, second, ALU.mult, op)
+            nc.sync.dma_start(out[:, targets(chunk)], result[:])
+
+        partial = sbuf("partial", 2 * P)
+        fused(partial[:, targets(1)], clipped_first[:], 0.5, hi[:, targets(1)], ALU.mult, ALU.add)
+        fused(partial[:, targets(0)], clipped_second[:, targets(0)], 0.5, hi[:, targets(0)], ALU.mult, ALU.add)
+        finish(3, clipped_second[:, targets(1)], 0.5, partial[:, targets(1)], ALU.add)
+        finish(0, total0[:], -1.0, minus_centre0[:], ALU.subtract)
+        finish(1, total1[:], 0.5, minus_centre1[:], ALU.subtract)
+        finish(2, total2[:], 0.5, partial[:, targets(0)], ALU.add)

@@ -46,7 +46,7 @@ def tile_picked_huber_none_p_kernel(tc, x_words, x_scales, w1, bound, offs, cen,
         scale_table = sbuf("scale_table", T, U8)
         identity = sbuf("identity", P)
         word_table = sbuf("word_table", T, U16)
-        b_col = sbuf("b_col", 3)
+        b_col = sbuf("b_col", 2)
         w_raw = keep.tile([P, PACK, N], F32, name="w_raw", tag="w_raw", align_bytes=64)
         bound_t = sbuf("bound_t", 2 * P)
         plane = sbuf("plane", S, U8)
@@ -63,7 +63,7 @@ def tile_picked_huber_none_p_kernel(tc, x_words, x_scales, w1, bound, offs, cen,
         nc.sync.dma_start(w_raw[:], w1.rearrange("(p t) n -> p t n", t=PACK))
         nc.sync.dma_start(bound_t[:], bound[:, targets(2, 2)])
         with nc.allow_non_contiguous_dma(reason="one bound to a partition"):
-            nc.sync.dma_start(b_col[:], bound[0, 0 : 3 * P].rearrange("(c p) -> p c", p=P))
+            nc.sync.dma_start(b_col[:], bound[0, 0 : 2 * P].rearrange("(c p) -> p c", p=P))
 
         w_bf = keep.tile([P, N, PACK], BF16, name="w_bf", align_bytes=64)
         w_codes = sbuf("w_codes", N, U32)
@@ -73,13 +73,11 @@ def tile_picked_huber_none_p_kernel(tc, x_words, x_scales, w1, bound, offs, cen,
         floor = sbuf("floor", 2 * P)
         nc.scalar.activation(floor[:], bound_t[:], ACT.Copy, scale=-2.0)
         minus_b = sbuf("minus_b", 2)
-        nc.scalar.activation(minus_b[:], b_col[:, 0:2], ACT.Copy, scale=-1.0)
+        nc.scalar.activation(minus_b[:], b_col[:], ACT.Copy, scale=-1.0)
         half_b = sbuf("half_b", 1)
         nc.scalar.activation(half_b[:], b_col[:, 0:1], ACT.Copy, scale=0.5)
         two_b = sbuf("two_b", 1)
         nc.scalar.activation(two_b[:], b_col[:, 1:2], ACT.Copy, scale=2.0)
-        floor_col = sbuf("floor_col", 1)
-        nc.scalar.activation(floor_col[:], b_col[:, 2:3], ACT.Copy, scale=-2.0)
 
         for first, count in ((0, 640), (640, 384)):
             picked = sbuf("scales%d" % first, count, U8)
@@ -147,7 +145,6 @@ def tile_picked_huber_none_p_kernel(tc, x_words, x_scales, w1, bound, offs, cen,
 
         diffs0 = (turned("diff_first0", "bank0", minus_centre0, first0), turned("diff_second0", "bank5", diff0))
         diffs1 = (turned("diff_first1", "bank1", minus_centre1, first1), turned("diff_second1", "bank7", minus_centre1, second1))
-        diff2 = turned("diff_first2", "bank4", below_first[:, targets(0)])
 
         def relu(name, source, bias, scale):
             made = sbuf(name, P)
@@ -159,27 +156,22 @@ def tile_picked_huber_none_p_kernel(tc, x_words, x_scales, w1, bound, offs, cen,
         rooms = [relu("room%d" % i, lifted[i], b_col[:, 0:1], -1.0) for i in range(2)]
         rooms.append(relu("room2", lifted[2], two_b[:], -1.0))
 
-        clipped_first = sbuf("clipped_first", P)
-        fused(clipped_first[:], below_first[:, targets(1)], 0.0, floor[:, targets(1)], ALU.min, ALU.max)
+        clipped_first = sbuf("clipped_first", 2 * P)
+        fused(clipped_first[:], below_first[:], 0.0, floor[:], ALU.min, ALU.max)
+        clip1 = sbuf("clip1", P)
+        nc.vector.tensor_scalar(clip1[:], diffs1[1][:], b_col[:, 1:2], minus_b[:, 1:2], ALU.min, ALU.max)
         clipped_second = sbuf("clipped_second", 2 * P)
         fused(clipped_second[:], below_second[:], 0.0, floor[:], ALU.min, ALU.max)
-        clip1 = below_first[:, targets(1)]
-        nc.vector.tensor_scalar(clip1, diffs1[1][:], b_col[:, 1:2], minus_b[:, 1:2], ALU.min, ALU.max)
-        clip2 = sbuf("clip2", P)
-        nc.vector.tensor_scalar(clip2[:], diff2[:], 0.0, floor_col[:], ALU.min, ALU.max)
         total0 = turned("total0", "bank6", minus_b[:, 0:1].to_broadcast([P, P]), rooms[0], rooms[1])
         total1 = turned("total1", "bank3", minus_b[:, 1:2].to_broadcast([P, P]), clip1, rooms[2])
-        total2 = turned("total2", "bank2", clip2)
 
-        def finish(chunk, first, scalar, second, op):
-            result = sbuf("result%d" % chunk, P)
+        def finish(chunk, chunks, first, scalar, second, op):
+            result = sbuf("result%d" % chunk, chunks * P)
             fused(result[:], first, scalar, second, ALU.mult, op)
-            nc.sync.dma_start(out[:, targets(chunk)], result[:])
+            nc.sync.dma_start(out[:, targets(chunk, chunks)], result[:])
 
         partial = sbuf("partial", 2 * P)
-        fused(partial[:, targets(1)], clipped_first[:], 0.5, hi[:, targets(1)], ALU.mult, ALU.add)
-        fused(partial[:, targets(0)], clipped_second[:, targets(0)], 0.5, hi[:, targets(0)], ALU.mult, ALU.add)
-        finish(3, clipped_second[:, targets(1)], 0.5, partial[:, targets(1)], ALU.add)
-        finish(0, total0[:], -1.0, minus_centre0[:], ALU.subtract)
-        finish(1, total1[:], 0.5, minus_centre1[:], ALU.subtract)
-        finish(2, total2[:], 0.5, partial[:, targets(0)], ALU.add)
+        fused(partial[:], clipped_first[:], 0.5, hi[:], ALU.mult, ALU.add)
+        finish(0, 1, total0[:], -1.0, minus_centre0[:], ALU.subtract)
+        finish(2, 2, clipped_second[:], 0.5, partial[:], ALU.add)
+        finish(1, 1, total1[:], 0.5, minus_centre1[:], ALU.subtract)

@@ -158,20 +158,22 @@ def tile_picked_huber_none_p_kernel(tc, x_words, x_scales, w1, bound, offs, cen,
 
         clipped_first = sbuf("clipped_first", 2 * P)
         fused(clipped_first[:], below_first[:], 0.0, floor[:], ALU.min, ALU.max)
-        clip1 = sbuf("clip1", P)
-        nc.vector.tensor_scalar(clip1[:], diffs1[1][:], b_col[:, 1:2], minus_b[:, 1:2], ALU.min, ALU.max)
         clipped_second = sbuf("clipped_second", 2 * P)
-        fused(clipped_second[:], below_second[:], 0.0, floor[:], ALU.min, ALU.max)
-        total0 = turned("total0", "bank6", minus_b[:, 0:1].to_broadcast([P, P]), rooms[0], rooms[1])
-        total1 = turned("total1", "bank3", minus_b[:, 1:2].to_broadcast([P, P]), clip1, rooms[2])
-
-        def finish(chunk, chunks, first, scalar, second, op):
-            result = sbuf("result%d" % chunk, chunks * P)
-            fused(result[:], first, scalar, second, ALU.mult, op)
-            nc.sync.dma_start(out[:, targets(chunk, chunks)], result[:])
-
         partial = sbuf("partial", 2 * P)
-        fused(partial[:], clipped_first[:], 0.5, hi[:], ALU.mult, ALU.add)
-        finish(0, 1, total0[:], -1.0, minus_centre0[:], ALU.subtract)
-        finish(2, 2, clipped_second[:], 0.5, partial[:], ALU.add)
-        finish(1, 1, total1[:], 0.5, minus_centre1[:], ALU.subtract)
+        clip1 = sbuf("clip1", P)
+        fused(clipped_second[:, targets(0)], below_second[:, targets(0)], 0.0, floor[:, targets(0)], ALU.min, ALU.max)
+        nc.vector.tensor_scalar(clip1[:], diffs1[1][:], b_col[:, 1:2], minus_b[:, 1:2], ALU.min, ALU.max)
+        fused(partial[:, targets(0)], clipped_first[:, targets(0)], 0.5, hi[:, targets(0)], ALU.mult, ALU.add)
+        fused(clipped_second[:, targets(1)], below_second[:, targets(1)], 0.0, floor[:, targets(1)], ALU.min, ALU.max)
+        fused(partial[:, targets(1)], clipped_first[:, targets(1)], 0.5, hi[:, targets(1)], ALU.mult, ALU.add)
+        total0 = turned("total0", "bank6", minus_b[:, 0:1].to_broadcast([P, P]), rooms[0], rooms[1])
+        total1 = turned("total1", "bank3", minus_b[:, 1:2].to_broadcast([P, P]), rooms[2], clip1)
+
+        def finish(chunk, result, first, scalar, second, op):
+            fused(result[:], first, scalar, second, ALU.mult, op)
+            nc.sync.dma_start(out[:, targets(chunk)], result[:])
+
+        finish(2, sbuf("result2", P), clipped_second[:, targets(0)], 0.5, partial[:, targets(0)], ALU.add)
+        finish(0, sbuf("result0", P), total0[:], -1.0, minus_centre0[:], ALU.subtract)
+        finish(3, rooms[1], clipped_second[:, targets(1)], 0.5, partial[:, targets(1)], ALU.add)
+        finish(1, sbuf("result1", P), total1[:], 0.5, minus_centre1[:], ALU.subtract)

@@ -20,7 +20,11 @@ ACT = mybir.ActivationFunctionType
 P = 128
 PACK = 4
 PER_COLUMN = 16
+QUADRANT = 32
 HALF = S // 2
+QUARTER = S // 4
+SCALE_ROW0 = P - K // 32
+SCALES_FIRST = 640
 
 
 def tile_picked_huber_none_p_kernel(tc, x_words, x_scales, w1, bound, offs, cen, pos1, pos2, out):
@@ -51,10 +55,10 @@ def tile_picked_huber_none_p_kernel(tc, x_words, x_scales, w1, bound, offs, cen,
         bound_t = sbuf("bound_t", 2 * P)
         plane = sbuf("plane", S, U8)
 
-        nc.vector.memset(scale_table[0:112, :].bitcast(I32), 0)
+        nc.vector.memset(scale_table[0:SCALE_ROW0, :].bitcast(I32), 0)
         nc.vector.memset(plane[:].bitcast(I32), 0)
         make_identity(nc, identity[:])
-        nc.sync.dma_start(scale_table[112:P, :].bitcast(I32), x_scales[0].bitcast(I32))
+        nc.sync.dma_start(scale_table[SCALE_ROW0:P, :].bitcast(I32), x_scales[0].bitcast(I32))
         nc.sync.dma_start(offs_t[:], offs)
         nc.sync.dma_start(cen_t[:], cen)
         nc.sync.dma_start(pos1_t[:], pos1)
@@ -70,20 +74,20 @@ def tile_picked_huber_none_p_kernel(tc, x_words, x_scales, w1, bound, offs, cen,
         w_scales = sbuf("w_scales", N, U8)
         nc.scalar.activation(w_bf[:], w_raw[:].rearrange("p t n -> p n t"), ACT.Copy)
 
-        floor = sbuf("floor", 2 * P)
-        nc.scalar.activation(floor[:], bound_t[:], ACT.Copy, scale=-2.0)
-        minus_b = sbuf("minus_b", 2)
-        nc.scalar.activation(minus_b[:], b_col[:], ACT.Copy, scale=-1.0)
-        half_b = sbuf("half_b", 1)
-        nc.scalar.activation(half_b[:], b_col[:, 0:1], ACT.Copy, scale=0.5)
-        two_b = sbuf("two_b", 1)
-        nc.scalar.activation(two_b[:], b_col[:, 1:2], ACT.Copy, scale=2.0)
+        def scaled(name, source, columns, factor):
+            made = sbuf(name, columns)
+            nc.scalar.activation(made[:], source, ACT.Copy, scale=factor)
+            return made
 
-        for first, count in ((0, 640), (640, 384)):
+        floor = scaled("floor", bound_t[:], 2 * P, -2.0)
+        minus_b = scaled("minus_b", b_col[:], 2, -1.0)
+        half_b = scaled("half_b", b_col[:, 0:1], 1, 0.5)
+
+        for first, count in ((0, SCALES_FIRST), (SCALES_FIRST, S - SCALES_FIRST)):
             picked = sbuf("scales%d" % first, count, U8)
             nc.vector.tensor_copy(picked[:], scale_table[:].indirect(entries(offs_t, first, count)))
             for r in range(4):
-                nc.sync.dma_start(plane[r:P:32, first : first + count].bitcast(I32), picked[112 + r : P : 4, :].bitcast(I32))
+                nc.sync.dma_start(plane[r:P:QUADRANT, first : first + count].bitcast(I32), picked[SCALE_ROW0 + r : P : 4, :].bitcast(I32))
 
         y = sbuf("y", S)
         words = [sbuf("words0", HALF, U16)]
@@ -99,15 +103,12 @@ def tile_picked_huber_none_p_kernel(tc, x_words, x_scales, w1, bound, offs, cen,
                                 start=True, stop=True)
             return acc
 
-        for first in (512, 768):
-            nc.vector.tensor_copy(words[1][:, first - HALF : first - HALF + 256], word_table[:].indirect(entries(offs_t, first, 256)))
-        for bank, first, count in (("bank0", 0, 256), ("bank1", 256, 256), ("bank4", 512, 128), ("bank5", 640, 128), ):
+        for first in (HALF, HALF + QUARTER):
+            nc.vector.tensor_copy(words[1][:, first - HALF : first - HALF + QUARTER], word_table[:].indirect(entries(offs_t, first, QUARTER)))
+        for bank, first, count in (("bank0", 0, QUARTER), ("bank1", QUARTER, QUARTER), ("bank4", HALF, P), ("bank5", SCALES_FIRST, P)):
             nc.scalar.activation(y[:, first : first + count], product(bank, first, count)[:], ACT.Copy)
-        nc.vector.tensor_copy(y[:, 768:896], product("bank2", 768, 128)[:])
-        nc.scalar.activation(y[:, 896:1024], product("bank3", 896, 128)[:], ACT.Copy)
-
-        def turn(bank, source, start=True, stop=True):
-            nc.tensor.matmul(bank, source, identity[:], start=start, stop=stop, is_transpose=True)
+        nc.vector.tensor_copy(y[:, S - 2 * P : S - P], product("bank2", S - 2 * P, P)[:])
+        nc.scalar.activation(y[:, S - P : S], product("bank3", S - P, P)[:], ACT.Copy)
 
         def picked_from_y(list_tile, chunk, chunks=1):
             return y[:].indirect(entries(list_tile, chunk * P, chunks * P))
@@ -120,60 +121,56 @@ def tile_picked_huber_none_p_kernel(tc, x_words, x_scales, w1, bound, offs, cen,
         def vector_gather(into, list_tile, chunk, chunks, other, op):
             nc.vector.tensor_tensor(into, picked_from_y(list_tile, chunk, chunks), other, op)
 
-        def fused(into, first, scalar, second, op0, op1):
-            nc.vector.scalar_tensor_tensor(into, first, scalar, second, op0, op1)
-
-        hi = sbuf("hi", 2 * P)
-        vector_gather(hi[:], cen_t, 2, 2, bound_t[:], ALU.add)
-        minus_centre0 = scalar_gather("minus_centre0", cen_t, 0, -1.0)
-        minus_centre1 = scalar_gather("minus_centre1", cen_t, 1, -1.0)
-        first0 = scalar_gather("first0", pos1_t, 0)
-        first1 = scalar_gather("first1", pos1_t, 1)
-        second1 = scalar_gather("second1", pos2_t, 1)
-        diff0 = sbuf("diff0", P)
-        vector_gather(diff0[:], pos2_t, 0, 1, minus_centre0[:], ALU.add)
-        below_first = sbuf("below_first", 2 * P)
-        vector_gather(below_first[:], pos1_t, 2, 2, hi[:], ALU.subtract)
-        below_second = sbuf("below_second", 2 * P)
-        vector_gather(below_second[:], pos2_t, 2, 2, hi[:], ALU.subtract)
+        def fused(into, tensor0, scalar, tensor1, op0, op1):
+            nc.vector.scalar_tensor_tensor(into, tensor0, scalar, tensor1, op0, op1)
 
         def turned(name, bank, *summands):
             held = psum.tile([P, P], F32, name=name, tag=bank)
             for place, summand in enumerate(summands):
-                turn(held[:], summand[:], start=place == 0, stop=place == len(summands) - 1)
+                nc.tensor.matmul(held[:], summand[:], identity[:], start=place == 0, stop=place == len(summands) - 1, is_transpose=True)
             return held
-
-        diffs0 = (turned("diff_first0", "bank0", minus_centre0, first0), turned("diff_second0", "bank5", diff0))
-        diffs1 = (turned("diff_first1", "bank1", minus_centre1, first1), turned("diff_second1", "bank7", minus_centre1, second1))
 
         def relu(name, source, bias, scale):
             made = sbuf(name, P)
             nc.scalar.activation(made[:], source[:], ACT.Relu, bias=bias, scale=scale)
             return made
 
-        lifted = [relu("lifted%d" % i, diffs0[i], half_b[:], 0.5) for i in range(2)]
-        lifted.append(relu("lifted2", diffs1[0], b_col[:, 1:2], -1.0))
-        rooms = [relu("room%d" % i, lifted[i], b_col[:, 0:1], -1.0) for i in range(2)]
-        rooms.append(relu("room2", lifted[2], two_b[:], -1.0))
+        hi = sbuf("hi", 2 * P)
+        for i in range(2):
+            vector_gather(hi[:, targets(i)], cen_t, 2 + i, 1, bound_t[:, targets(i)], ALU.add)
+        minus_centre = [scalar_gather("minus_centre%d" % chunk, cen_t, chunk, -1.0) for chunk in range(2)]
+        neighbours = [[scalar_gather("neighbour%d%d" % (chunk, d), list_tile, chunk) for d, list_tile in enumerate((pos1_t, pos2_t))]
+                      for chunk in range(2)]
+        below_first = sbuf("below_first", 2 * P)
+        for i in range(2):
+            vector_gather(below_first[:, targets(i)], pos1_t, 2 + i, 1, hi[:, targets(i)], ALU.subtract)
+        below_second = sbuf("below_second", 2 * P)
+        vector_gather(below_second[:], pos2_t, 2, 2, hi[:], ALU.subtract)
+
+        diffs = [[turned("diff%d%d" % (chunk, d), bank, minus_centre[chunk], neighbours[chunk][d]) for d, bank in enumerate(banks)]
+                 for chunk, banks in enumerate((("bank0", "bank5"), ("bank1", "bank7")))]
+
+        lifted = [relu("lifted%d" % d, diffs[0][d], half_b[:], 0.5) for d in range(2)]
+        rooms = [relu("room%d" % d, lifted[d], b_col[:, 0:1], -1.0) for d in range(2)]
 
         clipped_first = sbuf("clipped_first", 2 * P)
         fused(clipped_first[:], below_first[:], 0.0, floor[:], ALU.min, ALU.max)
         clipped_second = sbuf("clipped_second", 2 * P)
+        fused(clipped_second[:], below_second[:], 0.0, floor[:], ALU.min, ALU.max)
         partial = sbuf("partial", 2 * P)
-        clip1 = sbuf("clip1", P)
-        fused(clipped_second[:, targets(0)], below_second[:, targets(0)], 0.0, floor[:, targets(0)], ALU.min, ALU.max)
-        nc.vector.tensor_scalar(clip1[:], diffs1[1][:], b_col[:, 1:2], minus_b[:, 1:2], ALU.min, ALU.max)
-        fused(partial[:, targets(0)], clipped_first[:, targets(0)], 0.5, hi[:, targets(0)], ALU.mult, ALU.add)
-        fused(clipped_second[:, targets(1)], below_second[:, targets(1)], 0.0, floor[:, targets(1)], ALU.min, ALU.max)
-        fused(partial[:, targets(1)], clipped_first[:, targets(1)], 0.5, hi[:, targets(1)], ALU.mult, ALU.add)
+        clips1 = sbuf("clips1", 2 * P)
+        for i in range(2):
+            fused(partial[:, targets(i)], clipped_first[:, targets(i)], 0.5, hi[:, targets(i)], ALU.mult, ALU.add)
+            nc.vector.tensor_scalar(clips1[:, targets(i)], diffs[1][i][:], b_col[:, 1:2], minus_b[:, 1:2], ALU.min, ALU.max)
         total0 = turned("total0", "bank6", minus_b[:, 0:1].to_broadcast([P, P]), rooms[0], rooms[1])
-        total1 = turned("total1", "bank3", minus_b[:, 1:2].to_broadcast([P, P]), rooms[2], clip1)
+        total1 = turned("total1", "bank2", clips1[:, targets(0)], clips1[:, targets(1)])
 
-        def finish(chunk, result, first, scalar, second, op):
-            fused(result[:], first, scalar, second, ALU.mult, op)
+        def finish(chunk, term, factor, rest, op):
+            result = sbuf("result%d" % chunk, P)
+            fused(result[:], term, factor, rest, ALU.mult, op)
             nc.sync.dma_start(out[:, targets(chunk)], result[:])
 
-        finish(2, sbuf("result2", P), clipped_second[:, targets(0)], 0.5, partial[:, targets(0)], ALU.add)
-        finish(0, sbuf("result0", P), total0[:], -1.0, minus_centre0[:], ALU.subtract)
-        finish(3, rooms[1], clipped_second[:, targets(1)], 0.5, partial[:, targets(1)], ALU.add)
-        finish(1, sbuf("result1", P), total1[:], 0.5, minus_centre1[:], ALU.subtract)
+        for i in range(2):
+            finish(2 + i, clipped_second[:, targets(i)], 0.5, partial[:, targets(i)], ALU.add)
+        finish(0, total0[:], -1.0, minus_centre[0][:], ALU.subtract)
+        finish(1, total1[:], 0.5, minus_centre[1][:], ALU.subtract)

@@ -21,8 +21,6 @@ P = 128
 PACK = 4
 PER_COLUMN = 16
 QUADRANT = 32
-HALF = S // 2
-QUARTER = S // 4
 SCALE_ROW0 = P - K // 32
 SCALES_FIRST = 640
 
@@ -43,35 +41,33 @@ def tile_picked_huber_none_p_kernel(tc, x_words, x_scales, w1, bound, offs, cen,
         def targets(chunk, chunks=1):
             return slice(chunk * P, (chunk + chunks) * P)
 
-        offs_t = lists.tile([P, S // PER_COLUMN], U16, name="offs_t")
-        cen_t = lists.tile([P, V // PER_COLUMN], U16, name="cen_t")
-        pos1_t = lists.tile([P, V // PER_COLUMN], U16, name="pos1_t")
-        pos2_t = lists.tile([P, V // PER_COLUMN], U16, name="pos2_t")
-        scale_table = sbuf("scale_table", T, U8)
-        identity = sbuf("identity", P)
-        word_table = sbuf("word_table", T, U16)
-        b_col = sbuf("b_col", 2)
-        w_raw = keep.tile([P, PACK, N], F32, name="w_raw", tag="w_raw", align_bytes=64)
-        bound_t = sbuf("bound_t", 2 * P)
-        plane = sbuf("plane", S, U8)
+        def load_list(name, source, count):
+            held = lists.tile([P, count // PER_COLUMN], U16, name=name)
+            nc.sync.dma_start(held[:], source)
+            return held
 
+        scale_table = sbuf("scale_table", T, U8)
+        plane = sbuf("plane", S, U8)
+        identity = sbuf("identity", P)
         nc.vector.memset(scale_table[0:SCALE_ROW0, :].bitcast(I32), 0)
         nc.vector.memset(plane[:].bitcast(I32), 0)
         make_identity(nc, identity[:])
+
         nc.sync.dma_start(scale_table[SCALE_ROW0:P, :].bitcast(I32), x_scales[0].bitcast(I32))
-        nc.sync.dma_start(offs_t[:], offs)
-        nc.sync.dma_start(cen_t[:], cen)
-        nc.sync.dma_start(pos1_t[:], pos1)
-        nc.sync.dma_start(pos2_t[:], pos2)
-        nc.sync.dma_start(word_table[:].bitcast(I32), x_words[0].bitcast(I32))
+        offs_t = load_list("offs_t", offs, S)
+        cen_t = load_list("cen_t", cen, V)
+        pos_t = [load_list("pos1_t", pos1, V), load_list("pos2_t", pos2, V)]
+        w_raw = keep.tile([P, PACK, N], F32, name="w_raw", tag="w_raw", align_bytes=64)
         nc.sync.dma_start(w_raw[:], w1.rearrange("(p t) n -> p t n", t=PACK))
+        word_table = sbuf("word_table", T, U16)
+        nc.sync.dma_start(word_table[:].bitcast(I32), x_words[0].bitcast(I32))
+        bound_t = sbuf("bound_t", 2 * P)
         nc.sync.dma_start(bound_t[:], bound[:, targets(2, 2)])
+        b_col = sbuf("b_col", 2)
         with nc.allow_non_contiguous_dma(reason="one bound to a partition"):
             nc.sync.dma_start(b_col[:], bound[0, 0 : 2 * P].rearrange("(c p) -> p c", p=P))
 
         w_bf = keep.tile([P, N, PACK], BF16, name="w_bf", align_bytes=64)
-        w_codes = sbuf("w_codes", N, U32)
-        w_scales = sbuf("w_scales", N, U8)
         nc.scalar.activation(w_bf[:], w_raw[:].rearrange("p t n -> p n t"), ACT.Copy)
 
         def scaled(name, source, columns, factor):
@@ -81,7 +77,7 @@ def tile_picked_huber_none_p_kernel(tc, x_words, x_scales, w1, bound, offs, cen,
 
         floor = scaled("floor", bound_t[:], 2 * P, -2.0)
         minus_b = scaled("minus_b", b_col[:], 2, -1.0)
-        half_b = scaled("half_b", b_col[:, 0:1], 1, 0.5)
+        twice_b = scaled("twice_b", b_col[:], 2, 2.0)
 
         for first, count in ((0, SCALES_FIRST), (SCALES_FIRST, S - SCALES_FIRST)):
             picked = sbuf("scales%d" % first, count, U8)
@@ -89,26 +85,25 @@ def tile_picked_huber_none_p_kernel(tc, x_words, x_scales, w1, bound, offs, cen,
             for r in range(4):
                 nc.sync.dma_start(plane[r:P:QUADRANT, first : first + count].bitcast(I32), picked[SCALE_ROW0 + r : P : 4, :].bitcast(I32))
 
-        y = sbuf("y", S)
-        words = [sbuf("words0", HALF, U16)]
-        nc.vector.tensor_copy(words[0][:], word_table[:].indirect(entries(offs_t, 0, HALF)))
+        w_codes = sbuf("w_codes", N, U32)
+        w_scales = sbuf("w_scales", N, U8)
         nc.vector.quantize_mx(out=w_codes[:].bitcast(FP8X4), scales=w_scales[:], in_=w_bf[:].rearrange("p n t -> p (n t)"))
-        words.append(sbuf("words1", HALF, U16, tag="w_raw"))
+        words = sbuf("words", S, U16, tag="w_raw")
+        for first, count in ((0, 4 * P), (4 * P, 2 * P), (6 * P, 2 * P)):
+            nc.vector.tensor_copy(words[:, first : first + count], word_table[:].indirect(entries(offs_t, first, count)))
 
         def product(bank, first, count):
             acc = psum.tile([P, count], F32, name="acc%d" % first, tag=bank)
-            cols = slice(first % HALF, first % HALF + count)
+            cols = slice(first, first + count)
             nc.tensor.matmul_mx(out=acc[:], lhsT=w_codes[:].bitcast(FP8X4), lhsT_scale=w_scales[:],
-                                rhs=words[first // HALF][:, cols].bitcast(FP4X4), rhs_scale=plane[:, first : first + count],
-                                start=True, stop=True)
+                                rhs=words[:, cols].bitcast(FP4X4), rhs_scale=plane[:, cols], start=True, stop=True)
             return acc
 
-        for first in (HALF, HALF + QUARTER):
-            nc.vector.tensor_copy(words[1][:, first - HALF : first - HALF + QUARTER], word_table[:].indirect(entries(offs_t, first, QUARTER)))
-        for bank, first, count in (("bank0", 0, QUARTER), ("bank1", QUARTER, QUARTER), ("bank4", HALF, P), ("bank5", SCALES_FIRST, P)):
+        y = sbuf("y", S)
+        for bank, first, count in (("bank0", 0, 2 * P), ("bank1", 2 * P, 2 * P), ("bank4", 4 * P, P), ("bank5", 5 * P, P)):
             nc.scalar.activation(y[:, first : first + count], product(bank, first, count)[:], ACT.Copy)
-        nc.vector.tensor_copy(y[:, S - 2 * P : S - P], product("bank2", S - 2 * P, P)[:])
-        nc.scalar.activation(y[:, S - P : S], product("bank3", S - P, P)[:], ACT.Copy)
+        nc.vector.tensor_copy(y[:, 6 * P : 7 * P], product("bank2", 6 * P, P)[:])
+        nc.scalar.activation(y[:, 7 * P : S], product("bank3", 7 * P, P)[:], ACT.Copy)
 
         def picked_from_y(list_tile, chunk, chunks=1):
             return y[:].indirect(entries(list_tile, chunk * P, chunks * P))
@@ -117,9 +112,6 @@ def tile_picked_huber_none_p_kernel(tc, x_words, x_scales, w1, bound, offs, cen,
             made = sbuf(name, P)
             nc.scalar.activation(made[:], picked_from_y(list_tile, chunk), ACT.Copy, scale=scale)
             return made
-
-        def vector_gather(into, list_tile, chunk, chunks, other, op):
-            nc.vector.tensor_tensor(into, picked_from_y(list_tile, chunk, chunks), other, op)
 
         def fused(into, tensor0, scalar, tensor1, op0, op1):
             nc.vector.scalar_tensor_tensor(into, tensor0, scalar, tensor1, op0, op1)
@@ -130,47 +122,46 @@ def tile_picked_huber_none_p_kernel(tc, x_words, x_scales, w1, bound, offs, cen,
                 nc.tensor.matmul(held[:], summand[:], identity[:], start=place == 0, stop=place == len(summands) - 1, is_transpose=True)
             return held
 
-        def relu(name, source, bias, scale):
+        def on_scalar(name, source, func, bias, scale):
             made = sbuf(name, P)
-            nc.scalar.activation(made[:], source[:], ACT.Relu, bias=bias, scale=scale)
+            nc.scalar.activation(made[:], source[:], func, bias=bias, scale=scale)
             return made
 
         hi = sbuf("hi", 2 * P)
+        below = [sbuf("below%d" % d, 2 * P) for d in range(2)]
         for i in range(2):
-            vector_gather(hi[:, targets(i)], cen_t, 2 + i, 1, bound_t[:, targets(i)], ALU.add)
-        minus_centre = [scalar_gather("minus_centre%d" % chunk, cen_t, chunk, -1.0) for chunk in range(2)]
-        neighbours = [[scalar_gather("neighbour%d%d" % (chunk, d), list_tile, chunk) for d, list_tile in enumerate((pos1_t, pos2_t))]
-                      for chunk in range(2)]
-        below_first = sbuf("below_first", 2 * P)
+            nc.vector.tensor_tensor(hi[:, targets(i)], picked_from_y(cen_t, 2 + i), bound_t[:, targets(i)], ALU.add)
         for i in range(2):
-            vector_gather(below_first[:, targets(i)], pos1_t, 2 + i, 1, hi[:, targets(i)], ALU.subtract)
-        below_second = sbuf("below_second", 2 * P)
-        vector_gather(below_second[:], pos2_t, 2, 2, hi[:], ALU.subtract)
+            nc.vector.tensor_tensor(below[0][:, targets(i)], picked_from_y(pos_t[0], 2 + i), hi[:, targets(i)], ALU.subtract)
+        nc.vector.tensor_tensor(below[1][:], picked_from_y(pos_t[1], 2, 2), hi[:], ALU.subtract)
 
-        diffs = [[turned("diff%d%d" % (chunk, d), bank, minus_centre[chunk], neighbours[chunk][d]) for d, bank in enumerate(banks)]
-                 for chunk, banks in enumerate((("bank0", "bank5"), ("bank1", "bank7")))]
+        minus_centre = sbuf("minus_centre", 2 * P)
+        nc.scalar.activation(minus_centre[:], picked_from_y(cen_t, 0, 2), ACT.Copy, scale=-1.0)
+        neighbours = [[scalar_gather("neighbour%d%d" % (d, chunk), pos_t[d], chunk) for chunk in range(2)] for d in range(2)]
+        diffs = [[turned("diff%d%d" % (d, chunk), bank, minus_centre[:, targets(chunk)], neighbours[d][chunk]) for chunk, bank in enumerate(banks)]
+                 for d, banks in enumerate((("bank0", "bank1"), ("bank4", "bank5")))]
 
-        lifted = [relu("lifted%d" % d, diffs[0][d], half_b[:], 0.5) for d in range(2)]
-        rooms = [relu("room%d" % d, lifted[d], b_col[:, 0:1], -1.0) for d in range(2)]
+        rooms = [on_scalar("room%d" % chunk, diffs[0][chunk], ACT.Relu, b_col[:, chunk : chunk + 1], -1.0) for chunk in range(2)]
+        lifted = [on_scalar("lifted%d" % chunk, rooms[chunk], ACT.Relu, twice_b[:, chunk : chunk + 1], -1.0) for chunk in range(2)]
 
-        clipped_first = sbuf("clipped_first", 2 * P)
-        fused(clipped_first[:], below_first[:], 0.0, floor[:], ALU.min, ALU.max)
-        clipped_second = sbuf("clipped_second", 2 * P)
-        fused(clipped_second[:], below_second[:], 0.0, floor[:], ALU.min, ALU.max)
-        partial = sbuf("partial", 2 * P)
-        clips1 = sbuf("clips1", 2 * P)
+        clipped = [sbuf("clipped%d" % d, 2 * P) for d in range(2)]
+        for d in range(2):
+            fused(clipped[d][:], below[d][:], 0.0, floor[:], ALU.min, ALU.max)
+        clips = sbuf("clips", 2 * P)
+        partial = neighbours[1]
         for i in range(2):
-            fused(partial[:, targets(i)], clipped_first[:, targets(i)], 0.5, hi[:, targets(i)], ALU.mult, ALU.add)
-            nc.vector.tensor_scalar(clips1[:, targets(i)], diffs[1][i][:], b_col[:, 1:2], minus_b[:, 1:2], ALU.min, ALU.max)
-        total0 = turned("total0", "bank6", minus_b[:, 0:1].to_broadcast([P, P]), rooms[0], rooms[1])
-        total1 = turned("total1", "bank2", clips1[:, targets(0)], clips1[:, targets(1)])
+            nc.vector.tensor_scalar(clips[:, targets(i)], diffs[1][i][:], b_col[:, i : i + 1], minus_b[:, i : i + 1], ALU.min, ALU.max)
+            fused(partial[i][:], clipped[0][:, targets(i)], 0.5, hi[:, targets(i)], ALU.mult, ALU.add)
 
-        def finish(chunk, term, factor, rest, op):
+        totals = [turned("total%d" % chunk, bank, minus_b[:, chunk : chunk + 1].to_broadcast([P, P]), lifted[chunk], clips[:, targets(chunk)])
+                  for chunk, bank in enumerate(("bank6", "bank7"))]
+
+        def finish(chunk, term, rest, op):
             result = sbuf("result%d" % chunk, P)
-            fused(result[:], term, factor, rest, ALU.mult, op)
+            fused(result[:], term, 0.5, rest, ALU.mult, op)
             nc.sync.dma_start(out[:, targets(chunk)], result[:])
 
         for i in range(2):
-            finish(2 + i, clipped_second[:, targets(i)], 0.5, partial[:, targets(i)], ALU.add)
-        finish(0, total0[:], -1.0, minus_centre[0][:], ALU.subtract)
-        finish(1, total1[:], 0.5, minus_centre[1][:], ALU.subtract)
+            finish(2 + i, clipped[1][:, targets(i)], partial[i][:], ALU.add)
+        for chunk in range(2):
+            finish(chunk, totals[chunk][:], minus_centre[:, targets(chunk)], ALU.subtract)

@@ -23,6 +23,7 @@ PER_COLUMN = 16
 QUADRANT = 32
 SCALE_ROW0 = P - K // 32
 SCALES_FIRST = 640
+BLOCK = 8
 
 
 def tile_picked_huber_none_p_kernel(tc, x_words, x_scales, w1, bound, offs, cen, pos1, pos2, out):
@@ -60,12 +61,16 @@ def tile_picked_huber_none_p_kernel(tc, x_words, x_scales, w1, bound, offs, cen,
         w_raw = keep.tile([P, PACK, N], F32, name="w_raw", tag="w_raw", align_bytes=64)
         nc.sync.dma_start(w_raw[:], w1.rearrange("(p t) n -> p t n", t=PACK))
         word_table = sbuf("word_table", T, U16)
-        nc.sync.dma_start(word_table[:].bitcast(I32), x_words[0].bitcast(I32))
+        for first in range(0, T // 2, T // 4):
+            nc.sync.dma_start(word_table[:].bitcast(I32)[:, first : first + T // 4], x_words[0].bitcast(I32)[:, first : first + T // 4])
         bound_t = sbuf("bound_t", 2 * P)
-        nc.sync.dma_start(bound_t[:], bound[:, targets(2, 2)])
-        b_col = sbuf("b_col", 2)
-        with nc.allow_non_contiguous_dma(reason="one bound to a partition"):
-            nc.sync.dma_start(b_col[:], bound[0, 0 : 2 * P].rearrange("(c p) -> p c", p=P))
+        for i in range(2):
+            nc.sync.dma_start(bound_t[:, targets(i)], bound[:, targets(2 + i)])
+        b_padded = sbuf("b_padded", 2 * BLOCK)
+        b_col = b_padded[:, 0 : 2 * BLOCK : BLOCK]
+        for chunk in range(2):
+            with nc.allow_non_contiguous_dma(reason="one bound to a partition"):
+                nc.sync.dma_start(b_col[:, chunk : chunk + 1], bound[0, targets(chunk)].rearrange("(p c) -> p c", c=1))
 
         w_bf = keep.tile([P, N, PACK], BF16, name="w_bf", align_bytes=64)
         nc.scalar.activation(w_bf[:], w_raw[:].rearrange("p t n -> p n t"), ACT.Copy)
@@ -76,8 +81,8 @@ def tile_picked_huber_none_p_kernel(tc, x_words, x_scales, w1, bound, offs, cen,
             return made
 
         floor = scaled("floor", bound_t[:], 2 * P, -2.0)
-        minus_b = scaled("minus_b", b_col[:], 2, -1.0)
-        twice_b = scaled("twice_b", b_col[:], 2, 2.0)
+        minus_b = scaled("minus_b", b_col, 2, -1.0)
+        twice_b = scaled("twice_b", b_col, 2, 2.0)
 
         for first, count in ((0, SCALES_FIRST), (SCALES_FIRST, S - SCALES_FIRST)):
             picked = sbuf("scales%d" % first, count, U8)

@@ -61,8 +61,7 @@ def tile_picked_huber_none_p_kernel(tc, x_words, x_scales, w1, bound, offs, cen,
         w_raw = keep.tile([P, PACK, N], F32, name="w_raw", tag="w_raw", align_bytes=64)
         nc.sync.dma_start(w_raw[:], w1.rearrange("(p t) n -> p t n", t=PACK))
         word_table = sbuf("word_table", T, U16)
-        for first in range(0, T // 2, T // 4):
-            nc.sync.dma_start(word_table[:].bitcast(I32)[:, first : first + T // 4], x_words[0].bitcast(I32)[:, first : first + T // 4])
+        nc.sync.dma_start(word_table[:].bitcast(I32), x_words[0].bitcast(I32))
         bound_t = sbuf("bound_t", 2 * P)
         for i in range(2):
             nc.sync.dma_start(bound_t[:, targets(i)], bound[:, targets(2 + i)])

@@ -57,11 +57,11 @@ def tile_picked_huber_none_p_kernel(tc, x_words, x_scales, w1, bound, offs, cen,
         nc.sync.dma_start(scale_table[SCALE_ROW0:P, :].bitcast(I32), x_scales[0].bitcast(I32))
         offs_t = load_list("offs_t", offs, S)
         cen_t = load_list("cen_t", cen, V)
-        pos_t = [load_list("pos1_t", pos1, V), load_list("pos2_t", pos2, V)]
         w_raw = keep.tile([P, PACK, N], F32, name="w_raw", tag="w_raw", align_bytes=64)
         nc.sync.dma_start(w_raw[:], w1.rearrange("(p t) n -> p t n", t=PACK))
         word_table = sbuf("word_table", T, U16)
         nc.sync.dma_start(word_table[:].bitcast(I32), x_words[0].bitcast(I32))
+        pos_t = [load_list("pos1_t", pos1, V), load_list("pos2_t", pos2, V)]
         bound_t = sbuf("bound_t", 2 * P)
         for i in range(2):
             nc.sync.dma_start(bound_t[:, targets(i)], bound[:, targets(2 + i)])

@@ -62,14 +62,14 @@ def tile_picked_huber_none_p_kernel(tc, x_words, x_scales, w1, bound, offs, cen,
         word_table = sbuf("word_table", T, U16)
         nc.sync.dma_start(word_table[:].bitcast(I32), x_words[0].bitcast(I32))
         pos_t = [load_list("pos1_t", pos1, V), load_list("pos2_t", pos2, V)]
-        bound_t = sbuf("bound_t", 2 * P)
-        for i in range(2):
-            nc.sync.dma_start(bound_t[:, targets(i)], bound[:, targets(2 + i)])
         b_padded = sbuf("b_padded", 2 * BLOCK)
         b_col = b_padded[:, 0 : 2 * BLOCK : BLOCK]
         for chunk in range(2):
             with nc.allow_non_contiguous_dma(reason="one bound to a partition"):
                 nc.sync.dma_start(b_col[:, chunk : chunk + 1], bound[0, targets(chunk)].rearrange("(p c) -> p c", c=1))
+        bound_t = sbuf("bound_t", 2 * P)
+        for i in (1, 0):
+            nc.sync.dma_start(bound_t[:, targets(i)], bound[:, targets(2 + i)])
 
         w_bf = keep.tile([P, N, PACK], BF16, name="w_bf", align_bytes=64)
         nc.scalar.activation(w_bf[:], w_raw[:].rearrange("p t n -> p n t"), ACT.Copy)
@@ -80,6 +80,7 @@ def tile_picked_huber_none_p_kernel(tc, x_words, x_scales, w1, bound, offs, cen,
             return made
 
         floor = scaled("floor", bound_t[:], 2 * P, -2.0)
+        plus_b = scaled("plus_b", b_col, 2, 1.0)
         minus_b = scaled("minus_b", b_col, 2, -1.0)
         twice_b = scaled("twice_b", b_col, 2, 2.0)
 
@@ -154,7 +155,7 @@ def tile_picked_huber_none_p_kernel(tc, x_words, x_scales, w1, bound, offs, cen,
         clips = sbuf("clips", 2 * P)
         partial = neighbours[1]
         for i in range(2):
-            nc.vector.tensor_scalar(clips[:, targets(i)], diffs[1][i][:], b_col[:, i : i + 1], minus_b[:, i : i + 1], ALU.min, ALU.max)
+            nc.vector.tensor_scalar(clips[:, targets(i)], diffs[1][i][:], plus_b[:, i : i + 1], minus_b[:, i : i + 1], ALU.min, ALU.max)
             fused(partial[i][:], clipped[0][:, targets(i)], 0.5, hi[:, targets(i)], ALU.mult, ALU.add)
 
         totals = [turned("total%d" % chunk, bank, minus_b[:, chunk : chunk + 1].to_broadcast([P, P]), lifted[chunk], clips[:, targets(chunk)])

from contextlib import ExitStack

import concourse.mybir as mybir
from concourse.masks import make_identity

K, T, S, V, N = 512, 2048, 1024, 512, 128
FLOPS = 2 * K * N * S

F32 = mybir.dt.float32
BF16 = mybir.dt.bfloat16
I32 = mybir.dt.int32
U32 = mybir.dt.uint32
U16 = mybir.dt.uint16
U8 = mybir.dt.uint8
FP8X4 = mybir.dt.float8_e4m3fn_x4
FP4X4 = mybir.dt.float4_e2m1fn_x4
ALU = mybir.AluOpType
ACT = mybir.ActivationFunctionType

P = 128
PACK = 4
PER_COLUMN = 16
QUADRANT = 32
SCALE_ROW0 = P - K // 32
SCALES_FIRST = 640
BLOCK = 8


def tile_picked_huber_none_p_kernel(tc, x_words, x_scales, w1, bound, offs, cen, pos1, pos2, out):
    nc = tc.nc
    with ExitStack() as ctx:
        lists = ctx.enter_context(tc.tile_pool(name="lists", bufs=1))
        keep = ctx.enter_context(tc.tile_pool(name="keep", bufs=1))
        psum = ctx.enter_context(tc.psum_pool(name="psum", bufs=1))

        def sbuf(name, columns, dtype=F32, tag=None):
            return keep.tile([P, columns], dtype, name=name, tag=tag or name, align_bytes=64)

        def entries(list_tile, first, count):
            return list_tile[:, first // PER_COLUMN : (first + count) // PER_COLUMN]

        def targets(chunk, chunks=1):
            return slice(chunk * P, (chunk + chunks) * P)

        def load_list(name, source, count):
            held = lists.tile([P, count // PER_COLUMN], U16, name=name)
            nc.sync.dma_start(held[:], source)
            return held

        scale_table = sbuf("scale_table", T, U8)
        plane = sbuf("plane", S, U8)
        identity = sbuf("identity", P)
        nc.vector.memset(scale_table[0:SCALE_ROW0, :].bitcast(I32), 0)
        nc.vector.memset(plane[:].bitcast(I32), 0)
        make_identity(nc, identity[:])

        nc.sync.dma_start(scale_table[SCALE_ROW0:P, :].bitcast(I32), x_scales[0].bitcast(I32))
        offs_t = load_list("offs_t", offs, S)
        cen_t = load_list("cen_t", cen, V)
        w_raw = keep.tile([P, PACK, N], F32, name="w_raw", tag="w_raw", align_bytes=64)
        nc.sync.dma_start(w_raw[:], w1.rearrange("(p t) n -> p t n", t=PACK))
        word_table = sbuf("word_table", T, U16)
        nc.sync.dma_start(word_table[:].bitcast(I32), x_words[0].bitcast(I32))
        pos_t = [load_list("pos1_t", pos1, V), load_list("pos2_t", pos2, V)]
        b_padded = sbuf("b_padded", 2 * BLOCK)
        b_col = b_padded[:, 0 : 2 * BLOCK : BLOCK]
        for chunk in range(2):
            with nc.allow_non_contiguous_dma(reason="one bound to a partition"):
                nc.sync.dma_start(b_col[:, chunk : chunk + 1], bound[0, targets(chunk)].rearrange("(p c) -> p c", c=1))
        bound_t = sbuf("bound_t", 2 * P)
        for i in (1, 0):
            nc.sync.dma_start(bound_t[:, targets(i)], bound[:, targets(2 + i)])

        w_bf = keep.tile([P, N, PACK], BF16, name="w_bf", align_bytes=64)
        nc.scalar.activation(w_bf[:], w_raw[:].rearrange("p t n -> p n t"), ACT.Copy)

        def scaled(name, source, columns, factor):
            made = sbuf(name, columns)
            nc.scalar.activation(made[:], source, ACT.Copy, scale=factor)
            return made

        floor = scaled("floor", bound_t[:], 2 * P, -2.0)
        plus_b = scaled("plus_b", b_col, 2, 1.0)
        minus_b = scaled("minus_b", b_col, 2, -1.0)
        twice_b = scaled("twice_b", b_col, 2, 2.0)

        for first, count in ((0, SCALES_FIRST), (SCALES_FIRST, S - SCALES_FIRST)):
            picked = sbuf("scales%d" % first, count, U8)
            nc.vector.tensor_copy(picked[:], scale_table[:].indirect(entries(offs_t, first, count)))
            for r in range(4):
                nc.sync.dma_start(plane[r:P:QUADRANT, first : first + count].bitcast(I32), picked[SCALE_ROW0 + r : P : 4, :].bitcast(I32))

        w_codes = sbuf("w_codes", N, U32)
        w_scales = sbuf("w_scales", N, U8)
        nc.vector.quantize_mx(out=w_codes[:].bitcast(FP8X4), scales=w_scales[:], in_=w_bf[:].rearrange("p n t -> p (n t)"))
        words = sbuf("words", S, U16, tag="w_raw")
        for first, count in ((0, 4 * P), (4 * P, 2 * P), (6 * P, 2 * P)):
            nc.vector.tensor_copy(words[:, first : first + count], word_table[:].indirect(entries(offs_t, first, count)))

        def product(bank, first, count):
            acc = psum.tile([P, count], F32, name="acc%d" % first, tag=bank)
            cols = slice(first, first + count)
            nc.tensor.matmul_mx(out=acc[:], lhsT=w_codes[:].bitcast(FP8X4), lhsT_scale=w_scales[:],
                                rhs=words[:, cols].bitcast(FP4X4), rhs_scale=plane[:, cols], start=True, stop=True)
            return acc

        y = sbuf("y", S)
        for bank, first, count in (("bank0", 0, 2 * P), ("bank1", 2 * P, 2 * P), ("bank4", 4 * P, P), ("bank5", 5 * P, P)):
            nc.scalar.activation(y[:, first : first + count], product(bank, first, count)[:], ACT.Copy)
        nc.vector.tensor_copy(y[:, 6 * P : 7 * P], product("bank2", 6 * P, P)[:])
        nc.scalar.activation(y[:, 7 * P : S], product("bank3", 7 * P, P)[:], ACT.Copy)

        def picked_from_y(list_tile, chunk, chunks=1):
            return y[:].indirect(entries(list_tile, chunk * P, chunks * P))

        def scalar_gather(name, list_tile, chunk, scale=1.0):
            made = sbuf(name, P)
            nc.scalar.activation(made[:], picked_from_y(list_tile, chunk), ACT.Copy, scale=scale)
            return made

        def fused(into, tensor0, scalar, tensor1, op0, op1):
            nc.vector.scalar_tensor_tensor(into, tensor0, scalar, tensor1, op0, op1)

        def turned(name, bank, *summands):
            held = psum.tile([P, P], F32, name=name, tag=bank)
            for place, summand in enumerate(summands):
                nc.tensor.matmul(held[:], summand[:], identity[:], start=place == 0, stop=place == len(summands) - 1, is_transpose=True)
            return held

        def on_scalar(name, source, func, bias, scale):
            made = sbuf(name, P)
            nc.scalar.activation(made[:], source[:], func, bias=bias, scale=scale)
            return made

        hi = sbuf("hi", 2 * P)
        below = [sbuf("below%d" % d, 2 * P) for d in range(2)]
        for i in range(2):
            nc.vector.tensor_tensor(hi[:, targets(i)], picked_from_y(cen_t, 2 + i), bound_t[:, targets(i)], ALU.add)
        for i in range(2):
            nc.vector.tensor_tensor(below[0][:, targets(i)], picked_from_y(pos_t[0], 2 + i), hi[:, targets(i)], ALU.subtract)
        nc.vector.tensor_tensor(below[1][:], picked_from_y(pos_t[1], 2, 2), hi[:], ALU.subtract)

        minus_centre = sbuf("minus_centre", 2 * P)
        nc.scalar.activation(minus_centre[:], picked_from_y(cen_t, 0, 2), ACT.Copy, scale=-1.0)
        neighbours = [[scalar_gather("neighbour%d%d" % (d, chunk), pos_t[d], chunk) for chunk in range(2)] for d in range(2)]
        diffs = [[turned("diff%d%d" % (d, chunk), bank, minus_centre[:, targets(chunk)], neighbours[d][chunk]) for chunk, bank in enumerate(banks)]
                 for d, banks in enumerate((("bank0", "bank1"), ("bank4", "bank5")))]

        rooms = [on_scalar("room%d" % chunk, diffs[0][chunk], ACT.Relu, b_col[:, chunk : chunk + 1], -1.0) for chunk in range(2)]
        lifted = [on_scalar("lifted%d" % chunk, rooms[chunk], ACT.Relu, twice_b[:, chunk : chunk + 1], -1.0) for chunk in range(2)]

        clipped = [sbuf("clipped%d" % d, 2 * P) for d in range(2)]
        for d in range(2):
            fused(clipped[d][:], below[d][:], 0.0, floor[:], ALU.min, ALU.max)
        clips = sbuf("clips", 2 * P)
        partial = neighbours[1]
        for i in range(2):
            nc.vector.tensor_scalar(clips[:, targets(i)], diffs[1][i][:], plus_b[:, i : i + 1], minus_b[:, i : i + 1], ALU.min, ALU.max)
            fused(partial[i][:], clipped[0][:, targets(i)], 0.5, hi[:, targets(i)], ALU.mult, ALU.add)

        totals = [turned("total%d" % chunk, bank, minus_b[:, chunk : chunk + 1].to_broadcast([P, P]), lifted[chunk], clips[:, targets(chunk)])
                  for chunk, bank in enumerate(("bank6", "bank7"))]

        def finish(chunk, term, rest, op):
            result = sbuf("result%d" % chunk, P)
            fused(result[:], term, 0.5, rest, ALU.mult, op)
            nc.sync.dma_start(out[:, targets(chunk)], result[:])

        for i in range(2):
            finish(2 + i, clipped[1][:, targets(i)], partial[i][:], ALU.add)
        for chunk in range(2):
            finish(chunk, totals[chunk][:], minus_centre[:, targets(chunk)], ALU.subtract)
